import numpy as np, ml_dtypes
CORES = [3,11,19,27,35,43,51,59]
N = 8
BF = ml_dtypes.bfloat16
def gentries(a):
    return np.ascontiguousarray(a.reshape(8, 16, -1).transpose(0, 2, 1)).reshape(8, -1)
def gtable(e):
    e = np.asarray(e); return np.ascontiguousarray(e.reshape(8, -1, 16).transpose(0, 2, 1)).reshape(128, -1).astype(np.int32)
C, K0, NQ, T, L, DS, SB = 4096, 256, 256, 2, 3, 3, 14
KM = K0 + T * NQ
def machine(rng, k, p, q):
    cl = rng.permutation(np.concatenate([np.arange(k), rng.integers(0, k, C - k)]))
    o = np.argsort(cl, kind="stable"); size = np.bincount(cl, minlength=k); first = np.add.accumulate(size) - size
    x = rng.integers(0, k, (16, k))[:, cl]; nx = o[first[x] + rng.integers(0, size[x])]
    out = rng.integers(0, 16, (16, k))[:, cl]
    out = np.where(rng.random((16, C)) < p, rng.integers(0, 16, (16, C)), out)
    nx = np.where(rng.random((16, C)) < q, rng.integers(0, C, (16, C)), nx)
    return nx, out, cl
def machines(rng):
    nx = np.empty((N, 8, 16, C), np.int64); out = np.empty((N, 8, 16, C), np.int64)
    for r in range(N):
        for g in range(8):
            p = float(rng.choice(np.array([0.004, 0.01, 0.03])))
            nx[r, g], out[r, g], cl = machine(rng, int(rng.choice(np.array([30, 80, 200, 500]))), p, 0.3 * p)
    return nx, out
def others(rng):
    return (rng.integers(0, C, (N, 8, K0)), rng.integers(0, 2 ** SB, (N, 8, T, NQ)), rng.integers(0, 16, (N, 8, T, NQ)),
            rng.integers(0, 16, (N, 8, 16, L)), rng.integers(0, 16, (N, 8, T, 16, L)))
def fresh(rng, ex):
    b = C // (T + 1); c = np.arange(C)
    nx = rng.integers(0, C, (16, C)); out = rng.integers(0, 16, (16, C)); nx[15] = c
    for d in range(3): out[d] = (c >> (4 * d)) & 15
    for t in range(T): nx[3 + t] = (t + 1) * b + rng.integers(0, b, C)
    ex[13:] = 15; ex[13:, L - 1] = np.arange(3)
    return nx, out, rng.integers(0, b, K0), np.repeat(3 + np.arange(T), NQ).reshape(T, NQ)
def pack(nx, out, bk, qs, qc, ex, zs):
    return {"mt": np.ascontiguousarray(np.roll((16 * nx + out).reshape(N, 128, C), DS, axis=0)).astype(np.int32),
            "bk": np.stack([gtable(a) for a in bk]), "qs": np.stack([gtable(a.reshape(8, -1)) for a in qs]), "qc": np.stack([gtable(a.reshape(8, -1)) for a in qc]),
            "ex": np.ascontiguousarray(ex.reshape(N, 128, L)).astype(np.int32), "zs": np.ascontiguousarray(zs.transpose(0, 1, 3, 2, 4)).reshape(N, 128, T * L).astype(np.int32)}
def setup_inputs(rng):
    nx, out = machines(rng)
    return pack(nx, out, *others(rng))
def setup_inputs_grow(rng):
    nx, out = machines(rng); bk, qs, qc, ex, zs = others(rng); c = np.arange(C); h = C // 2
    for r in range(N):
        o = rng.permutation(8)
        for g in o[:3]: nx[r, g], out[r, g], bk[r, g], qc[r, g] = fresh(rng, ex[r, g])
        g = o[2]; nx[r, g, 4:3 + T] = np.where(c >= C // (T + 1), c, nx[r, g, 4:3 + T])
        qs[r, g, 1:, :8] = 2 ** SB - 1 - np.arange(8) * (2 ** SB // (K0 + NQ))
        for g in o[3:6]:
            k = int(rng.integers(20, 61)); nx[r, g], out[r, g], cl = machine(rng, k, 0.0, 0.0)
            one = np.unique(cl, return_index=True)[1]
            bk[r, g] = rng.permutation(np.concatenate([one, rng.integers(0, C, K0 - k)]))
        g = o[5]
        nx[r, g, 15] = c; out[r, g, 15] = np.where(c < h, 3, 9); nx[r, g, 14, :h] = rng.integers(h, C, h)
        one = np.unique(cl[:h], return_index=True)[1]
        bk[r, g] = rng.permutation(np.concatenate([one, rng.integers(0, h, K0 - len(one))]))
        qc[r, g, 0] = 14; ex[r, g] = rng.integers(0, 14, (16, L)); zs[r, g, 0, int(rng.integers(1, 16))] = 15
    return pack(nx, out, bk, qs, qc, ex, zs)
def setup_inputs_near(rng):
    nx = np.empty((N, 8, 16, C), np.int64); out = np.empty((N, 8, 16, C), np.int64); bk, qs, qc, ex, zs = others(rng)
    for r in range(N):
        for g in range(8):
            x, y, cl = machine(rng, 40, 0.0, 0.0); y = np.minimum(np.maximum(y, 1), 14); x[15] = np.arange(C)
            c = np.flatnonzero(rng.random(C) < 0.5); a = rng.integers(0, 16, len(c)); b = (a + rng.integers(1, 16, len(c))) & 15
            y[a, c] += 1
            if (r + g) & 1: y[b, c] -= 1
            nx[r, g] = x; out[r, g] = y; ex[r, g] = 15; ex[r, g, :, L - 1] = rng.permutation(16)
    return pack(nx, out, bk, qs, qc, ex, zs)
def setup_inputs_alike(rng):
    nx, out = machines(rng); bk, qs, qc, ex, zs = others(rng)
    bk[:, ::2] = np.take_along_axis(rng.integers(0, C, (N, 4, 6)), rng.integers(0, 6, (N, 4, K0)), 2)
    zs = np.take_along_axis(zs, rng.integers(0, 5, (N, 8, T, 16))[..., None], 3)
    ex[:, 1::4] = np.repeat(ex[:, 1::4, :4], 4, axis=2)
    qs[:, 3] = rng.integers(0, 2 ** SB, 4)[rng.integers(0, 4, (N, T, NQ))]; qc[:, 3] = rng.integers(0, 16, 2)[rng.integers(0, 2, (N, T, NQ))]
    for r in range(N):
        nx[r, 5], out[r, 5], bk[r, 5], qc[r, 5] = fresh(rng, ex[r, 5])
        qs[r, 5] = rng.integers(0, 2 ** SB, 3)[rng.integers(0, 3, (T, NQ))]
    c = np.arange(C)
    nx[:, 7] = np.where(rng.random((N, 16, C)) < 0.1, 0, rng.integers(0, C, (N, 16, C))); nx[:, 7, 15] = c
    out[:, 7] = np.where((c == 0) | (c >= C // 2), 0, rng.integers(1, 16, (N, 16, C)))
    out[1::2, 7] = 15 - out[1::2, 7]
    bk[:, 7] = rng.integers(1, C // 2, (N, K0)); qc[:, 7] = rng.integers(0, 15, (N, T, NQ))
    ex[:, 7] = 15; ex[:, 7, :, L - 1] = np.argsort(rng.random((N, 16)), axis=-1)
    for r in range(N):
        if r & 2:
            nx[r, 7, 14] = np.where(rng.random(C) < 0.5, bk[r, 7][rng.integers(0, K0, C)], rng.integers(1, C // 2, C))
            qc[r, 7, 0] = 14; zs[r, 7, :, :, :L - 1] = 15
    return pack(nx, out, bk, qs, qc, ex, zs)
def setup_inputs_ends(rng):
    nx, out = machines(rng); bk, qs, qc, ex, zs = others(rng); e = np.array([0, C - 1]); l = np.array([0, 15])
    nx = np.where(rng.random(nx.shape) < 0.2, e[rng.integers(0, 2, nx.shape)], nx)
    qs[:, ::2] = np.array([0, 2 ** SB - 1])[rng.integers(0, 2, (N, 4, T, NQ))]
    qs[:, 1::2, 0] = (rng.integers(0, K0, (N, 4, NQ)) * (2 ** SB // K0) - rng.integers(0, 2, (N, 4, NQ))) & (2 ** SB - 1)
    qc[:, 1] = l[rng.integers(0, 2, (N, T, NQ))]; bk[:, 2] = e[rng.integers(0, 2, (N, K0))]; bk[:, :, 0] = 0; bk[:, :, K0 - 1] = C - 1
    ex[:, 4] = l[rng.integers(0, 2, (N, 16, L))]; zs[:, 4] = l[rng.integers(0, 2, (N, T, 16, L))]; ex[:, 5] = 15; zs[:, 7] = 0
    return pack(nx, out, bk, qs, qc, ex, zs)
def setup_inputs_spread(rng):
    a = rng.choice(np.array([1, 3, 8]), (N, 8, 1, 1)); b = rng.choice(np.array([1, 2, 6]), (N, 8, 1, 1))
    nx = (C * rng.random((N, 8, 16, C)) ** a).astype(np.int64); out = (16 * rng.random((N, 8, 16, C)) ** b).astype(np.int64)
    bk = (C * rng.random((N, 8, K0)) ** a[..., 0]).astype(np.int64); qs = (2 ** SB * rng.random((N, 8, T, NQ)) ** b).astype(np.int64)
    qc = (16 * rng.random((N, 8, T, NQ)) ** 2).astype(np.int64)
    ex = (16 * rng.random((N, 8, 16, L)) ** 2).astype(np.int64); zs = (16 * rng.random((N, 8, T, 16, L)) ** 2).astype(np.int64)
    return pack(nx, out, bk, qs, qc, ex, zs)
def check_inputs(d):
    bad = []
    for k, hi in (("mt", 16 * C - 1), ("bk", C - 1), ("qs", 2 ** SB - 1), ("qc", 15), ("ex", 15), ("zs", 15)):
        if np.min(d[k]) < 0 or np.max(d[k]) > hi: bad.append("range of " + k)
    return bad
def walk(tb, q, w):
    r = np.arange(N)[:, None, None, None]; g = np.arange(8)[None, :, None, None]; s = q[:, :, None, :]
    for i in range(L):
        v = tb[r, g, w[:, :, :, i][..., None], s]; s = v >> 4
    return v & 15
def reference(mt, bk, qs, qc, ex, zs):
    tb = np.roll(mt.astype(np.int64), -DS, axis=0).reshape(N, 8, 16, C)
    s_ = np.stack([gentries(a) for a in qs]).astype(np.int64).reshape(N, 8, T, NQ); c_ = np.stack([gentries(a) for a in qc]).astype(np.int64).reshape(N, 8, T, NQ)
    E = ex.astype(np.int64).reshape(N, 8, 16, L); Z = zs.astype(np.int64).reshape(N, 8, 16, T, L)
    kn = np.zeros((N, 8, KM), np.int64); rec = np.zeros((N, 8, 16, KM), np.int64); cnt = np.full((N, 8, 1), K0, np.int64)
    kn[:, :, :K0] = np.stack([gentries(a) for a in bk]); rec[..., :K0] = walk(tb, kn[:, :, :K0], E)
    r3 = np.arange(N)[:, None, None]; g3 = np.arange(8)[None, :, None]; ms = []
    for t in range(T):
        b = np.take_along_axis(kn, (s_[:, :, t] * cnt) >> SB, 2)
        q = tb[r3, g3, c_[:, :, t], b] >> 4
        rq = walk(tb, q, E)
        eq = np.broadcast_to((np.arange(KM) < cnt)[:, :, None, :], (N, 8, NQ, KM))
        for e in range(16): eq = eq & (rq[:, :, e, :, None] == rec[:, :, e, None, :])
        hit = np.any(eq, axis=3); new = (~hit).astype(np.int64)
        m = np.where(hit, np.argmax(eq, axis=3), cnt + np.add.accumulate(new, axis=2) - new)
        i, j, n = np.nonzero(new)
        kn[i, j, m[i, j, n]] = q[i, j, n]; rec[i, j, :, m[i, j, n]] = rq[i, j, :, n]
        cnt = cnt + np.add.reduce(new, axis=2)[..., None]; ms.append(m)
        zt = Z[:, :, :, t]
        differ = walk(tb, q, zt) != walk(tb, np.take_along_axis(kn, m, 2), zt)
        best = np.argmax(np.add.reduce(differ.astype(np.int64), axis=3), axis=2)
        E[:, :, t] = zt[r3[..., 0], g3[..., 0], best]
        rec[:, :, t] = walk(tb, kn, E[:, :, t:t + 1])[:, :, 0]
    rec = np.where((np.arange(KM) < cnt)[:, :, None, :], rec, -1)
    return {"ym": np.concatenate(ms, axis=2).astype(np.float32), "yr": rec.reshape(N, 128, KM).astype(np.float32), "ye": E.reshape(N, 128, L).astype(np.float32)}

@@ -1,0 +1,529 @@
+from concourse.mybir import AluOpType as Alu, AxisListType as Ax, ActivationFunctionType as Act
+
+F32, BF, F16, I32, U16 = "float32", "bfloat16", "float16", "int32", "uint16"
+_SB = [("SIN", 89, I32), ("LIN", 89, I32), ("MT", 4096, I32), ("NX", 4096, F32), ("OT", 4096, BF),
+       ("IPI", 1, I32), ("PCI", 2, I32), ("PCF", 2, F32), ("TK", 1, F32), ("EF", 2, F32),
+       ("ICF", 128, BF), ("G16", 128, BF), ("C16", 128, BF), ("PRI", 128, BF), ("IDN", 128, BF), ("PRM", 128, BF),
+       ("IC16", 128, BF), ("BO", 128, BF), ("BON", 128, BF), ("M16", 128, BF), ("TRI", 128, BF), ("IM", 256, BF),
+       ("DB", 144, BF), ("KC", 256, F32), ("TBC", 16, BF), ("ZOI", 16, I32), ("ZOU", 16, U16), ("J16", 16, F32),
+       ("NN", 16, F32), ("CB", 16, F32), ("SL", 48, F32),
+       ("LU", 48, U16), ("KI", 32, I32), ("KU", 32, U16), ("WF", 25, F32), ("SP", 16, F32), ("MSK", 512, BF),
+       ("PT", 768, BF), ("P2C", 384, BF), ("W0", 3, F32), ("R24", 24, BF), ("SOF", 24, U16),
+       ("ZE", 4224, BF), ("ZA2", 2304, BF), ("ZA3", 2048, BF), ("ZB2", 2048, BF), ("ZB3", 2048, BF), ("ZQ", 2048, BF),
+       ("KG", 768, F32), ("GQ", 256, F32), ("G1U", 768, U16), ("HM", 512, F16), ("QU", 32, U16),
+       ("G2", 12288, F16), ("X3", 2048, U16), ("G3", 28672, BF),
+       ("REC", 528, BF), ("SA", 528, BF), ("KR", 784, BF), ("KS", 784, BF), ("TQ", 256, BF), ("TS", 256, BF), ("RQ1", 256, BF),
+       ("OWN", 512, BF), ("ZZ", 1152, BF), ("NPG", 1, F32), ("TK2", 1, F32),
+       ("SQ0", 528, BF), ("SQ1", 528, BF), ("SQQ", 256, BF), ("DBT", 768, F32), ("SCN", 8192, F32),
+       ("HL", 2, F32), ("UP", 32, F32), ("TT", 32, F32), ("NEW", 32, BF), ("HIT", 32, F32), ("INC", 36, F16), ("YY", 32, F32),
+       ("HD", 32, F32), ("SCF", 16, F32), ("SCU", 16, U16), ("CMF", 32, F32), ("CMU", 32, U16), ("MSG", 48, F16),
+       ("C1", 1, F32), ("NE", 512, BF), ("NC", 2, F32), ("RH", 32, BF), ("MN", 2, F32), ("WS", 256, BF),
+       ("PJ", 20, I32), ("PU", 10, U16),
+       ("RKR", 1040, BF), ("RKS", 1040, BF), ("RQ", 256, BF), ("RS", 256, BF), ("RMS", 48, F16), ("RWS", 128, BF),
+       ("RSU", 16, U16), ("FIN", 784, F32), ("YM", 512, F32)]
+SCRATCH = {n: ("sbuf", [128, w], d) for n, w, d in _SB}
+for _b in range(8):
+    SCRATCH["PS%d" % _b] = ("psum", [128, 512], F32)
+NCH = 8
+SEMAPHORES = (["cv", "ca", "cp", "cg", "lsem"] + ["d%d" % i for i in range(NCH + 8)] + ["r%d" % i for i in range(8)])
+
+CBIG = 201326592.0
+CY = 0.83e-3 * 1.2
+PEC = 0.42e-3 * 1.2
+CG, CS, LAT = 1.56, 3.8, 0.11
+ORDER = """
+0 20 1 19 2 13 3 4 5 6 7 15 8 9 24a 45v 16 22v 10 21a 28 27 25 29 14 23v 12 53 36a 11 32 33 37 66 67 69 60 56 68 70 17 72 47
+71 73 91 75 59 97 94 39 74 100 76 35 78 30 31 77 65 38 101 102 106 79 90 103 105 81 95 84 41 82 87 92 83 125 104 124 88 107
+80 108 34 131a 93 110 85 111 112 132 126 137a 113 89 133 44 63 143 138 109 114 115 127 149a 139 86 144 119 116 51 128 134
+118 145 129 120 150 117 184a 46 135 140v 244 155 136 146 141 42 151 166 156 142 152 147 48 157 245 167 172 148 158 153 50
+250 168 40 178 154 173 169 18 43 159 174 49 251 179 175v 160 121 246 170 180 247v 185 171 181 176 256 52 186 177v 161 188v
+182 122 187 162 252v 183 98 54 189 248 190 163 191 58 62 192 130 257 197 195 253 193 198 196 201 199 202 263 200 249v 258
+26 123 203 205 254 204 264 206 96 207 259 209 208 210 211 164 213 212 214 215 165 99 217 216 55 194 61 218 255 219 266 221
+220 222 223 225 224 260 226 265 227 228 295 233 241 242 229 231 230 232 261 296 262 234 236 298 235 267 237 243 301 268v
+270 238 269 297 240 274 271 275 302 276 272 304 277 273 299 278 321 308 303 280 279 281 322 284 300 323a 305 282 309 283
+324 310 325 314 326 285 327v 328 286 331 332 287v 329 333 288 336 306v 330v 289 337 334 339v 338 290 335v 315 291 307 340
+343 341 311 358 342 294 362 364 316 363 312 365 366 344 313v 368 359 350 369 345 367 372 292 239 370 373 317 371 376 377
+374 375 380 346 381 378 318 379 351 382 352 319v 384 383 347 320 385 386 353 388 387 360 389 390 391 392 348 349 293 393
+354 361 57 394 395 398 396 355 400 399 397 356 403 64 401 357 404 402 406 405 407 408 409 410 411 412 413 416 414 417 415
+419 422 420 423 421 418 424
+"""
+
+
+def build(T, topo, core):
+    n_ranks = len(T.cores)
+    rank = T.rank_of(core)
+    owner = T.cores[(rank + 3) % n_ranks]
+    client = T.cores[(rank - 3) % n_ranks]
+    ops = []
+    cnt = {"d": 0, "r": 0}
+
+    def ap(r):
+        if r[0] == "ind":
+            return ap(r[1]).indirect(ap(r[2]))
+        p = r[4] if len(r) > 4 else 128
+        if len(r) > 3 and r[3] != 1:
+            return T[r[0]][0:p, r[1]:r[2]:r[3]]
+        return T[r[0]][0:p, r[1]:r[2]]
+
+    def regs(rs):
+        out = []
+        for r in rs:
+            if isinstance(r, tuple):
+                out += [r[1], r[2]] if r[0] == "ind" else [r]
+        return out
+
+    def num(r):
+        if r[0] == "ind":
+            return 16 * (r[2][2] - r[2][1])
+        st = r[3] if len(r) > 3 else 1
+        return (r[2] - r[1] + st - 1) // st
+
+    def sc(x):
+        return ap(x) if isinstance(x, tuple) else x
+
+    def add(eng, fn, w, rd, occ, lat=None, kind="c", sem=None, n=1):
+        if w[0] == "ind":
+            rd = list(rd) + [w[2]]
+            w = w[1]
+        ops.append({"eng": eng, "fn": fn, "w": [w], "r": regs(rd), "occ": occ, "lat": occ if lat is None else lat,
+                    "kind": kind, "sem": sem, "n": n})
+
+    def vcost(o, ins, k):
+        if o[0] == "ind":
+            k = CS
+        elif ins[0][0] == "ind":
+            k = CG
+        return 0.06 + max(64, num(o) * k) * CY
+
+    def half(*rs):
+        return 0.5 if all(r[0] != "ind" and SCRATCH[r[0]][2] in (BF, F16, U16) for r in rs) else 1
+
+    def ts(o, i, s1, s2, op0, op1=None):
+        def fn(q, e):
+            if op1 is None:
+                return q.tensor_scalar(ap(o), ap(i), sc(s1), None, op0)
+            return q.tensor_scalar(ap(o), ap(i), sc(s1), sc(s2), op0, op1)
+        add("v", fn, o, [i, s1, s2], vcost(o, [i], half(o, i)))
+
+    def tt(o, a, b, op):
+        k = 1 if a[0].startswith("PS") or b[0].startswith("PS") else 2
+        add("v", lambda q, e: q.tensor_tensor(ap(o), ap(a), ap(b), op), o, [a, b], vcost(o, [a], k))
+
+    def cp(o, i, eng="v"):
+        def fn(q, e):
+            if e == "v":
+                return q.tensor_copy(ap(o), ap(i))
+            return q.activation(ap(o), ap(i), Act.Copy)
+        add(eng, fn, o, [i], vcost(o, [i], half(o, i) if eng == "v" else 1))
+
+    def act(o, i, func=Act.Identity, bias=0.0, scale=1.0):
+        add("a", lambda q, e: q.activation(ap(o), ap(i), func, bias=sc(bias), scale=sc(scale)), o, [i, bias, scale], vcost(o, [i], 1))
+
+    def ms(o, v):
+        add("v", lambda q, e: q.memset(ap(o), v), o, [], vcost(o, [o], half(o)))
+
+    def red(o, i, op, neg=False):
+        add("v", lambda q, e: q.tensor_reduce(ap(o), ap(i), Ax.X, op, negate=neg), o, [i], 0.06 + max(64, num(i)) * CY)
+
+    def scan(o, d0, d1, init, op0, op1):
+        add("v", lambda q, e: q.tensor_tensor_scan(ap(o), ap(d0), ap(d1), sc(init), op0, op1), o, [d0, d1, init], vcost(o, [d0], 1))
+
+    def mm(items):
+        def fn(q, e):
+            x = None
+            for o, l, r, a, b in items:
+                x = q.matmul(ap(o), ap(l), ap(r), a, b)
+            return x
+        rd = []
+        for it in items:
+            rd += [it[1], it[2]]
+        c = sum(max(64, num(it[2])) for it in items) * PEC
+        add("p", fn, items[0][0], rd, c, c + 0.05)
+
+    def acc(o, prs):
+        mm([(o, l, r, i == 0, i == len(prs) - 1) for i, (l, r) in enumerate(prs)])
+
+    def iota(o, pat, base, cm):
+        def fn(q, e):
+            if SCRATCH[o[0]][2] == I32:
+                return q.iota(ap(o), pat, base, cm)
+            return q.iota(ap(o), pat, base, cm, allow_small_or_imprecise_dtypes=True)
+        add("g", fn, o, [], 0.13 + 2 * num(o) * CY)
+
+    def pick(o, i, pat, op, cm):
+        add("g", lambda q, e: q.affine_select(ap(o), ap(i), pat, op, 0.0, 0, cm), o, [i], 0.17 + 256 * CY)
+
+    def fill1(o):
+        def fn(q, e):
+            if e == "v":
+                return q.memset(ap(o), 0.0)
+            if e == "a":
+                return q.activation(ap(o), T.ZZ[:, 0:num(o)], Act.Copy)
+            return q.iota(ap(o), [[0, num(o)]], 0, 0, allow_small_or_imprecise_dtypes=True)
+        add("gav", fn, o, [("ZZ", 0, 1152)], 0.13 + 2 * num(o) * CY)
+        ops[-1]["alt"] = {"v": 0.06 + 0.5 * num(o) * CY, "a": 0.07 + num(o) * CY}
+
+    def fill(name, lo, hi):
+        for a in range(lo, hi, 1152):
+            fill1((name, a, min(hi, a + 1152)))
+
+    def dma(eng, prs, w, rd, lat):
+        s = "d%d" % cnt["d"]
+        cnt["d"] += 1
+
+        def fn(q, e):
+            for o, i in prs:
+                q.dma_start(o, i).then_inc(T.sem[s], 16)
+        add(eng, fn, w, rd, 0.07 * len(prs), lat, "d", s, 16 * len(prs))
+
+    def send(dst, o, i, lat):
+        s = "r%d" % cnt["r"]
+        cnt["r"] += 1
+        rid, pid, _ = topo.addr(dst)
+        add("g", lambda q, e: q.remote_dma(ap(o), ap(i), T.sem[s], T.sem.lsem, pid, rid, topo.mask(core, dst)),
+            o, [i], 0.4, lat, "r", s, len(topo.engines(core, dst)))
+
+    def ind(w, o):
+        return ("ind", w, o)
+
+    def ps(b, lo, hi, st=1, p=128):
+        return ("PS%d" % b, lo, hi, st, p)
+
+    def dd(i):
+        return ("DB", 15 - i, 143 - i)
+
+    PI, PG = ("PCF", 0, 1), ("PCF", 1, 2)
+    E16 = ("M16", 0, 16)
+
+    dma("a", [(T.SIN[:, 0:16], T.bk[:, :]), (T.SIN[:, 16:48], T.qc[:, :]), (T.SIN[:, 48:80], T.qs[:, :])], ("SIN", 0, 80), [], 2.2)
+    dma("s", [(T.SIN[:, 80:83], T.ex[:, :]), (T.SIN[:, 83:89], T.zs[:, :])], ("SIN", 80, 89), [], 2.2)
+    cw = 4096 // NCH
+    for c in range(NCH):
+        dma("s", [(T.MT[:, c * cw:(c + 1) * cw], T.mt[:, c * cw:(c + 1) * cw])], ("MT", c * cw, (c + 1) * cw), [], 2.3 + (c + 1) * 7.0 / NCH)
+        ops[-1]["after"] = len(ops) - 2
+    iota(("IPI", 0, 1), [[0, 1]], 0, 1)
+    iota(("ICF", 0, 128), [[1, 128]], 0, 0)
+    iota(("G16", 0, 128), [[16, 8], [0, 16]], 0, 0)
+    iota(("C16", 0, 128), [[0, 8], [1, 16]], 0, 0)
+    send(owner, ("LIN", 0, 89), ("SIN", 0, 89), 4.0)
+    iota(("PRI", 0, 128), [[0, 128]], 1, 0)
+    pick(("IDN", 0, 128), ("PRI", 0, 128), [[-1, 128]], Alu.is_equal, 1)
+    pick(("PRM", 0, 128), ("PRI", 0, 128), [[-1, 16], [-16, 8]], Alu.is_equal, 1)
+    iota(("ZOI", 0, 16), [[128, 16]], 0, 1)
+    iota(("J16", 0, 16), [[16, 16]], 0, 0)
+    ms(("ZZ", 0, 1152), 0.0)
+    fill("ZE", 0, 4224)
+    ms(("DB", 0, 144), 0.0)
+    ms(("INC", 0, 1), 16.0)
+    ts(("PCI", 0, 1), ("IPI", 0, 1), 15, None, Alu.bitwise_and)
+    ts(("PCI", 1, 2), ("IPI", 0, 1), 112, None, Alu.bitwise_and)
+    cp(("PCF", 0, 2), ("PCI", 0, 2))
+    act(("NPG", 0, 1), PG, scale=-1.0)
+    act(("IC16", 0, 128), ("ICF", 0, 128), bias=("NPG", 0, 1))
+    ts(("BO", 0, 128), ("G16", 0, 128), PG, None, Alu.is_equal)
+    ts(("M16", 0, 128), ("C16", 0, 128), PI, None, Alu.is_equal)
+    fill("ZA2", 0, 2304)
+    fill("ZA3", 0, 2048)
+    cp(("DB", 15, 143, 16), ("BO", 0, 128, 16), "a")
+    act(("BON", 0, 128), ("BO", 0, 128), scale=-1.0)
+    pick(("TRI", 0, 128), ("BO", 0, 128), [[1, 128]], Alu.is_gt, -1)
+    fill("ZQ", 0, 2048)
+    iota(("KG", 256, 768), [[0, 512]], 0, 0)
+    fill("ZB2", 0, 2048)
+    fill("ZB3", 0, 2048)
+    iota(("KR", 272, 784), [[0, 512]], -1, 0)
+    iota(("KS", 272, 784), [[0, 512]], -1, 0)
+    iota(("RKR", 528, 1040), [[0, 512]], -1, 0)
+    iota(("RKS", 528, 1040), [[0, 512]], -1, 0)
+    cp(("ZOU", 0, 16), ("ZOI", 0, 16))
+    act(("NN", 0, 16), ("J16", 0, 16), bias=PI)
+    act(("CB", 0, 16), ("NN", 0, 16), bias=256.0, scale=1.0 / 512)
+    for k in range(3):
+        act(("SL", 16 * k, 16 * k + 16), ("NN", 0, 16), bias=256.0 * (k + 1))
+    act(("TK", 0, 1), PI, bias=1000.0, scale=1.0 / 8192)
+    act(("EF", 0, 2), ("M16", 0, 2), bias=1.0, scale=-1.0)
+    act(("TK2", 0, 1), PI, scale=1.0 / 8192)
+    act(("TBC", 0, 16), E16, scale=("TK2", 0, 1))
+    for t in range(2):
+        act(("KC", 128 * t, 128 * t + 128), dd(t), bias=-1000.0, scale=("TK", 0, 1))
+        act(("IM", 128 * t, 128 * t + 128), ("IDN", 0, 128), scale=("EF", t, t + 1))
+
+    for c in range(NCH):
+        lo, hi = c * cw, (c + 1) * cw
+        ts(("NX", lo, hi), ("MT", lo, hi), -7.5, CBIG, Alu.add, Alu.add)
+        act(ps(c % 2, 0, cw), ("NX", lo, hi), bias=-CBIG)
+        tt(("OT", lo, hi), ("MT", lo, hi), ps(c % 2, 0, cw), Alu.subtract)
+
+    cp(("LU", 0, 48), ("LIN", 0, 48))
+    cp(("WF", 0, 25), ("LIN", 64, 89))
+    ts(("KI", 0, 16), ("LIN", 48, 64), 6, None, Alu.arith_shift_right)
+    cp(("KU", 0, 16), ("KI", 0, 16))
+    act(("W0", 0, 3), ("WF", 16, 25, 3), bias=PG, scale=128.0)
+    cp(("MSK", 0, 512), ind(E16, ("LU", 16, 48)), "a")
+    act(("SP", 0, 16), ("WF", 0, 16), scale=1.0 / 16384)
+    cp(("REC", 0, 16), ("WF", 3, 19), "a")
+    cp(("SA", 0, 16), ("WF", 6, 22), "a")
+    cp(("KS", 0, 16), ("WF", 9, 25), "a")
+    for s in range(3):
+        act(("R24", 8 * s, 8 * s + 8), ("BO", 0, 128, 16), scale=("W0", s, s + 1))
+    acc(ps(2, 256, 280), [(("M16", 0, 128), ("R24", 0, 24))])
+    ts(("SOF", 0, 24), ps(2, 256, 280), PI, None, Alu.add)
+    Z2 = [("ZE", 0), ("ZA2", 0), ("ZB2", 0)]
+    Z3 = [("ZE", 2176), ("ZA3", 0), ("ZB3", 0)]
+
+    def selectors(s, b):
+        p2, p3 = ("PT", 256 * s, 256 * s + 128), ("PT", 256 * s + 128, 256 * s + 256)
+        ts(p2, ("IC16", 0, 128), ("WF", 17 + 3 * s, 18 + 3 * s), None, Alu.is_equal)
+        ts(p3, ("IC16", 0, 128), ("WF", 18 + 3 * s, 19 + 3 * s), None, Alu.is_equal)
+        it = [(ps(b, 0, 128), p2, ("IDN", 0, 128), True, True), (ps(b, 128, 256), p3, ("PRM", 0, 128), True, True)]
+        if s == 1:
+            it.append((ps(b, 256, 384), p3, ("IDN", 0, 128), True, True))
+        mm(it)
+        cp(("P2C", 128 * s, 128 * s + 128), ps(b, 0, 128), "a")
+        cp((Z3[s][0], Z3[s][1], Z3[s][1] + 2048, 16), ps(b, 128, 256), "a")
+        if s == 1:
+            cp(("ZA2", 2176, 2304), ps(b, 256, 384), "a")
+        cp(ind((Z2[s][0], 0, 2048), ("SOF", 8 * s, 8 * s + 8)), ("P2C", 128 * s, 128 * s + 128))
+
+    selectors(0, 2)
+    selectors(1, 7)
+    selectors(2, 7)
+    WNX, WOT = ("NX", 0, 4096), ("OT", 0, 4096)
+    CENTRE = -(CBIG / 16 + 2048.0)
+
+    def step1(lst, k0, keep):
+        ts(("G1U", k0, k0 + 256), ind(WNX, lst), CBIG, 1.0 / 16, Alu.subtract, Alu.mult)
+        if keep is not None:
+            act(keep, ind(WNX, lst), bias=CENTRE, scale=1.0 / 16)
+
+    def queries(t):
+        tt(("HM", 256 * t, 256 * t + 256), ind(("KG", 0, 256 * (t + 1)), ("KU", 16 * t, 16 * t + 16)), ("MSK", 256 * t, 256 * t + 256), Alu.mult)
+        acc(ps(2, 0, 16), [(dd(i), ("HM", 256 * t + i, 256 * t + 256, 16)) for i in range(16)])
+        ts(("QU", 16 * t, 16 * t + 16), ps(2, 0, 16), 2048.0, None, Alu.add)
+        step1(("QU", 16 * t, 16 * t + 16), 256 * (t + 1), ("GQ", 0, 256) if t == 0 else None)
+
+    def step2(k0, w):
+        o, i = ("G2", 16 * k0, 16 * (k0 + w)), ind(WNX, ("G1U", k0, k0 + w))
+
+        def fn(q, e):
+            if e == "v":
+                return q.tensor_scalar(ap(o), ap(i), CBIG + 32768.0, 1.0 / 16, Alu.subtract, Alu.mult)
+            return q.activation(ap(o), ap(i), Act.Identity, bias=CENTRE, scale=1.0 / 16)
+        add("va", fn, o, [i], vcost(o, [i], 1))
+
+    def dest(s, k):
+        if s == 0:
+            return ("REC", 16 + k) if k < 512 else ("RQ1", k - 512)
+        if s == 1:
+            return ("SA", 16 + k)
+        return ("KS", 16 + k) if k < 256 or k >= 512 else ("TS", k - 256)
+
+    def walk(s, k0, w, sub):
+        b2, b3 = (3, 4) if s == 0 else (5, 6)
+        x0 = (0, 768, 1280)[s] + k0
+        y0 = (k0 % 512, 512 + k0, 1024 + k0)[s]
+        z, o = Z2[s]
+        acc(ps(b2, 0, w), [((z, 128 * a, 128 * a + 128), ("G2", 16 * k0 + a, 16 * (k0 + w), 16)) for a in range(16)])
+        ts(("X3", x0, x0 + w), ps(b2, 0, w), 2048.0, None, Alu.add)
+        for u in range(0, w, sub):
+            cp(("G3", 16 * (y0 + u), 16 * (y0 + u + sub)), ind(WOT, ("X3", x0 + u, x0 + u + sub)), "av")
+        z, o = Z3[s]
+        acc(ps(b3, 0, w), [((z, o + 127 * e, o + 127 * e + 128), ("G3", 16 * y0 + e, 16 * (y0 + w), 16)) for e in range(16)])
+        d, c0 = dest(s, k0)
+        cp((d, c0, c0 + w), ps(b3, 0, w), "av")
+        if s and k0 >= 256 * s:
+            cp(("OWN", k0 - 256, k0 - 256 + w), ps(b3, 0, w), "av")
+
+    RT = 0.70710678
+
+    def known_side(t, src, sq):
+        n = 256 * (t + 1)
+        act((sq, 15, 16 + n), (src, 15, 16 + n), Act.Square, scale=RT)
+        acc(ps(7, 0, n), [(("BO", 0, 128), (sq, 16, 16 + n)), (("BON", 0, 128), (sq, 15, 15 + n))])
+        act(("DBT", 256 * t, 256 * t + n), ps(7, 0, n), bias=1.0 / 2048)
+        acc(ps(7, 0, 2), [(("BO", 0, 128), (sq, 14 + n, 16 + n))])
+        act(("HL", t, t + 1), ps(7, 1, 2), bias=(n - 1) / 2048.0)
+
+    def match(t, rq, sq, known):
+        n = 256 * (t + 1)
+        c = (16 * t, 16 * t + 16)
+        cp(ind(("ZQ", 0, 2048), ("ZOU", 0, 16)), rq)
+        act(sq, rq, Act.Square, scale=RT)
+        acc(ps(2, 0, 16), [(dd(i), (sq[0], sq[1] + i, sq[2], 16)) for i in range(16)])
+        act(("UP",) + c, ps(2, 0, 16), bias=("HL", t, t + 1))
+        for j in range(16):
+            acc(ps(j % 2, 0, n), [(("ZQ", 128 * j, 128 * j + 128), (known, 16, 16 + n))])
+            scan(("SCN", 512 * j, 512 * j + n), ("DBT", 256 * t, 256 * t + n), ps(j % 2, 0, n), -1.0e9, Alu.add, Alu.max)
+        tt(("TT",) + c, ("UP",) + c, ("SCN", n - 1, 8192, 512), Alu.subtract)
+        ts(("NEW",) + c, ("TT",) + c, 0.4, None, Alu.is_ge)
+        i0 = 18 * t
+        scan(("INC", i0 + 1, i0 + 17), ("NEW",) + c, ("NEW",) + c, 16.0 if t == 0 else ("C1", 0, 1), Alu.add, Alu.max)
+        mm([(ps(2, 0, 17), ("BO", 0, 128), ("INC", i0, i0 + 17), True, False), (ps(2, 0, 16), ("TRI", 0, 128), ("NEW",) + c, False, True)])
+        ts(("HIT",) + c, ("TT",) + c, 0.4, None, Alu.is_lt)
+        tt(("HD",) + c, ("HIT",) + c, ("SL", 16 * (t + 1), 16 * (t + 2)), Alu.mult)
+        ts(("YY",) + c, ("TT",) + c, 2048.0, None, Alu.mult)
+        if t == 0:
+            tt(("SCF", 0, 16), ("HD",) + c, ps(2, 0, 16), Alu.max)
+            cp(("SCU", 0, 16), ("SCF", 0, 16))
+            ts(("KI", 16, 32), ("SP", 0, 16), ps(2, 16, 17), -0.499969482421875, Alu.mult, Alu.add)
+            cp(("KU", 16, 32), ("KI", 16, 32))
+            act(("C1", 0, 1), ps(2, 16, 17), scale=1.0 / 16)
+            cp(("INC", 18, 19), ("C1", 0, 1))
+        else:
+            tt(("MSG", 32, 48), ("HD",) + c, ps(2, 0, 16), Alu.max)
+        tt(("MSG",) + c, ("YY",) + c, ps(2, 0, 16), Alu.min)
+        tt(("CMF",) + c, ("YY",) + c, ("SL",) + c, Alu.min)
+        cp(("CMU",) + c, ("CMF",) + c)
+
+    def winner(t, src):
+        n = 256 * (t + 1)
+        ne = ("NE", 256 * t, 256 * t + 256)
+        tt(ne, ind((src, 16, 272 + n), ("CMU", 16 * t, 16 * t + 16)), ("OWN", n - 256, n), Alu.not_equal)
+        red(("NC", t, t + 1), ne, Alu.add, True)
+        ts(("RH", 16 * t, 16 * t + 16), E16, ("NC", t, t + 1), None, Alu.mult)
+        acc(ps(2, 0, 16), [(("BO", 0, 128), ("RH", 16 * t, 16 * t + 16)), (("BO", 0, 128), ("TBC", 0, 16))])
+        red(("MN", t, t + 1), ps(2, 0, 16), Alu.min)
+        ts(("WS", 128 * t, 128 * t + 128), ("KC", 128 * t, 128 * t + 128), ("NC", t, t + 1), ("MN", t, t + 1), Alu.add, Alu.is_equal)
+
+    step1(("LU", 0, 16), 0, ("KG", 0, 256))
+    queries(0)
+    for k0, w, sub in ((0, 32, 32), (32, 32, 32), (64, 64, 64), (128, 64, 64), (192, 64, 64), (256, 64, 64), (320, 64, 64),
+                       (384, 64, 64), (448, 64, 32)):
+        step2(k0, w)
+        walk(0, k0, w, sub)
+        if k0 == 192:
+            known_side(0, "REC", "SQ0")
+    match(0, ("REC", 272, 528), ("SQ0", 272, 528), "REC")
+    cp(ind(("KG", 0, 768), ("SCU", 0, 16)), ("GQ", 0, 256))
+    for k0 in range(0, 512, 128):
+        walk(1, k0, 128, 64)
+    queries(1)
+    winner(0, "SA")
+    ts(("PJ", 0, 9), ("CB", 0, 9), ("MN", 0, 1), 8192.0, Alu.add, Alu.mult)
+    ts(("PJ", 10, 19), ("PJ", 0, 9), 8191, None, Alu.bitwise_and)
+    cp(("PU", 0, 9), ("PJ", 10, 19))
+    cp(("ZE", 0, 2304, 16), ind(("ZA2", 0, 2304), ("PU", 0, 9)))
+    acc(ps(7, 0, 256), [(("IM", 0, 128), ("REC", 272, 528)), (("WS", 0, 128), ("SA", 272, 528))])
+    cp(("TQ", 0, 256), ps(7, 0, 256), "av")
+    acc(ps(7, 0, 272), [(("IM", 0, 128), ("REC", 0, 272)), (("WS", 0, 128), ("SA", 0, 272))])
+    cp(("KR", 0, 272), ps(7, 0, 272), "av")
+    cp(ind(("KR", 16, 784), ("SCU", 0, 16)), ("TQ", 0, 256))
+    known_side(1, "KR", "SQ1")
+    send(client, ("RKR", 0, 528), ("KR", 0, 528), 4.5)
+    walk(2, 256, 128, 64)
+    walk(2, 384, 128, 64)
+    cp(ind(("KS", 16, 784), ("SCU", 0, 16)), ("TS", 0, 256))
+    walk(2, 0, 128, 64)
+    walk(2, 128, 128, 64)
+    send(client, ("RKS", 0, 528), ("KS", 0, 528), 4.5)
+    for k0 in range(512, 768, 64):
+        step2(k0, 64)
+    walk(0, 512, 128, 64)
+    walk(0, 640, 64, 64)
+    walk(0, 704, 64, 32)
+    send(client, ("RQ", 0, 256), ("RQ1", 0, 256), 3.5)
+    walk(2, 512, 128, 64)
+    walk(2, 640, 128, 64)
+    send(client, ("RS", 0, 256), ("OWN", 256, 512), 3.5)
+    match(1, ("RQ1", 0, 256), ("SQQ", 0, 256), "KR")
+    send(client, ("RMS", 0, 48), ("MSG", 0, 48), 2.5)
+    winner(1, "KS")
+    send(client, ("RWS", 0, 128), ("WS", 128, 256), 2.7)
+    cp(("RSU", 0, 16), ("RMS", 32, 48))
+    cp(ind(("RKR", 16, 1040), ("RSU", 0, 16)), ("RQ", 0, 256))
+    cp(ind(("RKS", 16, 1040), ("RSU", 0, 16)), ("RS", 0, 256))
+    mm([(ps(7, i, 512, 16, 8), ("IDN", i, 128, 16), ("RMS", 0, 32), True, True) for i in range(16)])
+    cp(("YM", 0, 512, 1, 8), ps(7, 0, 512, 1, 8), "a")
+    dma("s", [(T.ym[:, :], T.YM[0:8, :])], ("ym", 0, 512), [("YM", 0, 512)], 2.2)
+    for b, lo, hi, e, q in ((3, 0, 400, "v", "s"), (4, 400, 784, "a", "a")):
+        acc(ps(b, 0, hi - lo), [(("IM", 128, 256), ("RKR", lo, hi)), (("RWS", 0, 128), ("RKS", lo, hi))])
+        cp(("FIN", lo, hi), ps(b, 0, hi - lo), e)
+        a = max(lo, 16)
+        prs = [(T.yr[:, a - 16:hi - 16], T.FIN[:, a:hi])]
+        if lo == 0:
+            prs.append((T.ye[:, :], T.FIN[:, 13:16]))
+        dma(q, prs, ("yr", lo, hi), [("FIN", lo, hi)], 3.0)
+    return ops
+
+
+def deps(ops):
+    pred = [dict() for _ in ops]
+    seen = {}
+    for i, o in enumerate(ops):
+        use = [(r, True) for r in o["w"]] + [(r, False) for r in o["r"]]
+        for r, wr in use:
+            lst = seen.get(r[0], [])
+            if r[0].startswith("PS"):
+                if lst and lst[-1][0] != i:
+                    pred[i].setdefault(lst[-1][0], False)
+            else:
+                for j, lo, hi, w2 in lst:
+                    if j != i and lo < r[2] and r[1] < hi and (wr or w2):
+                        pred[i][j] = True
+        for r, wr in use:
+            seen.setdefault(r[0], []).append((i, r[1], r[2], wr))
+        if "after" in o:
+            pred[i].setdefault(o["after"], None)
+    return pred
+
+
+def rank_program(g, core, T, topo):
+    if T.rank_of(core) is None:
+        return
+    ops = build(T, topo, core)
+    pred = deps(ops)
+    seq = []
+    for x in ORDER.split():
+        i = int(x.rstrip("vag"))
+        ops[i]["on"] = x[-1] if x[-1] in "vag" else ops[i]["eng"][0]
+        seq.append(i)
+    pos = {i: k for k, i in enumerate(seq)}
+    assert sorted(seq) == list(range(len(ops)))
+    known = {e: {} for e in "vapgs"}
+    clock, waits, wanted = {}, {}, set()
+    for i in seq:
+        e = ops[i]["on"]
+        kn = known[e]
+        waits[i] = []
+        for j in sorted(pred[i], key=lambda j: -pos[j]):
+            assert pos[j] < pos[i]
+            w = pred[i][j]
+            pj = ops[j]
+            if w is None or (pj["on"] == e and pj["kind"] == "c" and (not w or e == "p")):
+                continue
+            key = pj["on"] if pj["kind"] == "c" else pj["sem"]
+            if kn.get(key, -1) >= pos[j]:
+                continue
+            waits[i].append(j)
+            wanted.add(j)
+            kn[key] = pos[j]
+            if pj["kind"] != "r":
+                for k2, v2 in clock[j].items():
+                    if kn.get(k2, -1) < v2:
+                        kn[k2] = v2
+        clock[i] = dict(kn)
+    count, total = {}, {e: 0 for e in "vapgs"}
+    for i in seq:
+        if ops[i]["kind"] == "c" and i in wanted:
+            total[ops[i]["on"]] += 1
+            count[i] = total[ops[i]["on"]]
+    queue = {"v": g.vector, "a": g.scalar, "p": g.tensor, "g": g, "s": g.sync}
+    sent = 0
+    for i in seq:
+        o = ops[i]
+        q = queue[o["on"]]
+        for j in waits[i]:
+            pj = ops[j]
+            if pj["kind"] == "c":
+                q.wait_ge(T.sem["c" + pj["on"]], count[j])
+            else:
+                q.wait_ge(T.sem[pj["sem"]], pj["n"])
+        x = o["fn"](q, o["on"])
+        if i in count:
+            x.then_inc(T.sem["c" + o["on"]], 1)
+        if o["kind"] == "r":
+            sent += o["n"]
+    g.wait_ge(T.sem.lsem, sent)
+    for i in seq:
+        if ops[i]["kind"] == "d" and i not in wanted:
+            g.sync.wait_ge(T.sem[ops[i]["sem"]], ops[i]["n"])

@@ -20,32 +20,32 @@ _SB = [("SIN", 89, I32), ("LIN", 89, I32), ("MT", 4096, I32), ("NX", 4096, F32),
        ("C1", 1, F32), ("NE", 512, BF), ("NC", 2, F32), ("RH", 32, BF), ("MN", 2, F32), ("WS", 256, BF),
        ("PJ", 20, I32), ("PU", 10, U16),
        ("RKR", 1040, BF), ("RKS", 1040, BF), ("RQ", 256, BF), ("RS", 256, BF), ("RMS", 48, F16), ("RWS", 128, BF),
-       ("RSU", 16, U16), ("FIN", 784, F32), ("YM", 512, F32)]
+       ("RSU", 16, U16), ("FIN", 784, F32), ("YM", 512, F32), ("FL", 768, F32), ("FE", 16, F32)]
 SCRATCH = {n: ("sbuf", [128, w], d) for n, w, d in _SB}
 for _b in range(8):
     SCRATCH["PS%d" % _b] = ("psum", [128, 512], F32)
 NCH = 8
-SEMAPHORES = (["cv", "ca", "cp", "cg", "lsem"] + ["d%d" % i for i in range(NCH + 8)] + ["r%d" % i for i in range(8)])
+SEMAPHORES = (["cv", "ca", "cp", "cg", "lsem"] + ["d%d" % i for i in range(NCH + 10)] + ["r%d" % i for i in range(8)])
 
 CBIG = 201326592.0
 CY = 0.83e-3 * 1.2
 PEC = 0.42e-3 * 1.2
 CG, CS, LAT = 1.56, 3.8, 0.11
 ORDER = """
-0 20 1 19 2 13 3 4 5 6 7 15 8 9 24a 45v 16 22v 10 21a 28 27 25 29 14 23v 12 53 36a 11 32 33 37 66 67 69 60 56 68 70 17 72 47
-71 73 91 75 59 97 94 39 74 100 76 35 78 30 31 77 65 38 101 102 106 79 90 103 105 81 95 84 41 82 87 92 83 125 104 124 88 107
-80 108 34 131a 93 110 85 111 112 132 126 137a 113 89 133 44 63 143 138 109 114 115 127 149a 139 86 144 119 116 51 128 134
-118 145 129 120 150 117 184a 46 135 140v 244 155 136 146 141 42 151 166 156 142 152 147 48 157 245 167 172 148 158 153 50
-250 168 40 178 154 173 169 18 43 159 174 49 251 179 175v 160 121 246 170 180 247v 185 171 181 176 256 52 186 177v 161 188v
-182 122 187 162 252v 183 98 54 189 248 190 163 191 58 62 192 130 257 197 195 253 193 198 196 201 199 202 263 200 249v 258
-26 123 203 205 254 204 264 206 96 207 259 209 208 210 211 164 213 212 214 215 165 99 217 216 55 194 61 218 255 219 266 221
-220 222 223 225 224 260 226 265 227 228 295 233 241 242 229 231 230 232 261 296 262 234 236 298 235 267 237 243 301 268v
-270 238 269 297 240 274 271 275 302 276 272 304 277 273 299 278 321 308 303 280 279 281 322 284 300 323a 305 282 309 283
-324 310 325 314 326 285 327v 328 286 331 332 287v 329 333 288 336 306v 330v 289 337 334 339v 338 290 335v 315 291 307 340
-343 341 311 358 342 294 362 364 316 363 312 365 366 344 313v 368 359 350 369 345 367 372 292 239 370 373 317 371 376 377
-374 375 380 346 381 378 318 379 351 382 352 319v 384 383 347 320 385 386 353 388 387 360 389 390 391 392 348 349 293 393
-354 361 57 394 395 398 396 355 400 399 397 356 403 64 401 357 404 402 406 405 407 408 409 410 411 412 413 416 414 417 415
-419 422 420 423 421 418 424
+20 1 10 0 12 2 3 4 5 6 19 7 28 8 9 13 27 22a 29 15 32 11 33 25 23v 16 38 60 58 36v 24a 14 48 30 53 66 46 67 69 31 68 70 72
+56 35 71 73 90 75 95 92 91 78 76 17 74 54 59 21 55 77 96 99 39 94 106 81 102 100 62 105 101 93 82 84 103 79 87 37 97 104
+111 125 112 107 124 113 108 83 109 131a 110 34 126 88 132 80 137a 89 114 133 115 143 116 47 138 85 127 149a 139 86 144 43
+117 134 128 145 244 155 45 130 146 150 135 245 151 44 140v 156 136 152 129 141 157 118 166 250 142 158 18 41 147 172 167
+148 184a 153 168 119 42 178 120 173 154 246 159 251 40 174 247v 179 49 169 256 50 160v 180 175v 121 181 170 51 185 171v
+186 257 161 176 188v 122 162 177 187 52 252v 182 183 163 189 258 164 248 190v 26 191 63 253 123 199 195 197 263 200 196
+198 192 249v 201 259 207 205 264 203 202 254 208 206 204 209 165 213 266 255v 215 211 210 193 216 217 212 223 214 219 218
+194 221 61 224 265 225 220 260 222 226 295 227 261v 228 231 233 229 232 262v 230 241 296 267 234 236 235 238 237 298 242
+243 301 268v 240 269v 297 270 274 271 302 275 272 304 276 273 277 299 278 321 308 303 280 300v 322 323a 305 281 309 282
+279 310 283 284 324 325 98 314 326 285v 328 327v 331 286 332 287v 329 333 315 306v 288 336 330v 337 294 289 307 334 338
+290 339v 343 335 311 317v 340 341 291 312 358 316 344 313v 368 362 366 369 359 364 346 350 367 365 374 363 376 372 345
+351 375 370 318 373 377 380 319 292 382 371 384 293 320 353 381 342 378 383 388 379 390 352 347 389 385 386 391 348 392
+349 360 387 354 393 361 57 394 239 355 395 400 356 398 64 396 403 65 399 397 404 401 402 406 405 407 357 408 409 410 411
+412 416 413 414 417 418 420 415 419 422 421 428 423 425 429 424v 430 426 427
 """
 
 
@@ -352,8 +352,9 @@ def build(T, topo, core):
         acc(ps(2, 0, 16), [(dd(i), (sq[0], sq[1] + i, sq[2], 16)) for i in range(16)])
         act(("UP",) + c, ps(2, 0, 16), bias=("HL", t, t + 1))
         for j in range(16):
-            acc(ps(j % 2, 0, n), [(("ZQ", 128 * j, 128 * j + 128), (known, 16, 16 + n))])
-            scan(("SCN", 512 * j, 512 * j + n), ("DBT", 256 * t, 256 * t + n), ps(j % 2, 0, n), -1.0e9, Alu.add, Alu.max)
+            b = (0, 1, 3, 4)[j % 4]
+            acc(ps(b, 0, n), [(("ZQ", 128 * j, 128 * j + 128), (known, 16, 16 + n))])
+            scan(("SCN", 512 * j, 512 * j + n), ("DBT", 256 * t, 256 * t + n), ps(b, 0, n), -1.0e9, Alu.add, Alu.max)
         tt(("TT",) + c, ("UP",) + c, ("SCN", n - 1, 8192, 512), Alu.subtract)
         ts(("NEW",) + c, ("TT",) + c, 0.4, None, Alu.is_ge)
         i0 = 18 * t
@@ -435,14 +436,18 @@ def build(T, topo, core):
     mm([(ps(7, i, 512, 16, 8), ("IDN", i, 128, 16), ("RMS", 0, 32), True, True) for i in range(16)])
     cp(("YM", 0, 512, 1, 8), ps(7, 0, 512, 1, 8), "a")
     dma("s", [(T.ym[:, :], T.YM[0:8, :])], ("ym", 0, 512), [("YM", 0, 512)], 2.2)
-    for b, lo, hi, e, q in ((3, 0, 400, "v", "s"), (4, 400, 784, "a", "a")):
-        acc(ps(b, 0, hi - lo), [(("IM", 128, 256), ("RKR", lo, hi)), (("RWS", 0, 128), ("RKS", lo, hi))])
-        cp(("FIN", lo, hi), ps(b, 0, hi - lo), e)
-        a = max(lo, 16)
-        prs = [(T.yr[:, a - 16:hi - 16], T.FIN[:, a:hi])]
-        if lo == 0:
-            prs.append((T.ye[:, :], T.FIN[:, 13:16]))
-        dma(q, prs, ("yr", lo, hi), [("FIN", lo, hi)], 3.0)
+    cp(("FIN", 16, 400), ("RKR", 16, 400), "av")
+    cp(("FIN", 400, 784), ("RKR", 400, 784), "av")
+    rows = [(0, 1)] + [(16 * k + 2, min(16 * k + 17, 128)) for k in range(8)]
+    for q, part in (("s", rows[:5]), ("a", rows[5:])):
+        dma(q, [(T.yr[a:b, :], T.FIN[a:b, 16:784]) for a, b in part], ("yr" + q, 0, 1), [("FIN", 16, 784)], 3.2)
+    for b, lo in ((3, 0), (4, 384)):
+        acc(ps(b, 0, 384, 1, 8), [(("RWS", 1, 128, 16), ("RKS", 16 + lo, 400 + lo))])
+        cp(("FL", lo, lo + 384, 1, 8), ps(b, 0, 384, 1, 8), "av")
+    dma("s", [(T.yr[1:128:16, :], T.FL[0:8, :])], ("yr1", 0, 1), [("FL", 0, 768)], 2.2)
+    acc(ps(2, 0, 16), [(("IM", 128, 256), ("RKR", 0, 16)), (("RWS", 0, 128), ("RKS", 0, 16))])
+    cp(("FE", 0, 16), ps(2, 0, 16), "av")
+    dma("s", [(T.ye[:, :], T.FE[:, 13:16])], ("ye", 0, 1), [("FE", 0, 16)], 2.2)
     return ops
 
 

@@ -1,51 +1,54 @@
 from concourse.mybir import AluOpType as Alu, AxisListType as Ax, ActivationFunctionType as Act
 
 F32, BF, F16, I32, U16 = "float32", "bfloat16", "float16", "int32", "uint16"
-_SB = [("SIN", 89, I32), ("LIN", 89, I32), ("MT", 4096, I32), ("NX", 4096, F32), ("OT", 4096, BF),
-       ("IPI", 1, I32), ("PCI", 2, I32), ("PCF", 2, F32), ("TK", 1, F32), ("EF", 2, F32),
-       ("ICF", 128, BF), ("G16", 128, BF), ("C16", 128, BF), ("PRI", 128, BF), ("IDN", 128, BF), ("PRM", 128, BF),
-       ("IC16", 128, BF), ("BO", 128, BF), ("BON", 128, BF), ("M16", 128, BF), ("TRI", 128, BF), ("IM", 256, BF),
-       ("DB", 144, BF), ("KC", 256, F32), ("TBC", 16, BF), ("ZOI", 16, I32), ("ZOU", 16, U16), ("J16", 16, F32),
-       ("NN", 16, F32), ("CB", 16, F32), ("SL", 48, F32),
+_SB = [("SIN", 89, I32), ("LIN", 89, I32), ("MT", 4096, I32), ("NX", 4096, I32),
+       ("PCI", 3, I32), ("PCF", 3, F32), ("TK", 1, F32), ("EF", 2, F32),
+       ("G16", 128, BF), ("C16", 128, BF), ("PRI", 128, BF), ("IDN", 128, BF),
+       ("BO", 128, BF), ("BON", 128, BF), ("M16", 128, BF), ("TRI", 128, BF), ("IM", 256, BF),
+       ("DB", 144, BF), ("KC", 256, F32), ("TBC", 16, BF), ("J16", 16, F32),
+       ("NN", 16, F32), ("CB", 16, F32), ("SLN", 32, F32), ("SLU", 32, F16),
        ("LU", 48, U16), ("KI", 32, I32), ("KU", 32, U16), ("WF", 25, F32), ("SP", 16, F32), ("MSK", 512, BF),
-       ("PT", 768, BF), ("P2C", 384, BF), ("W0", 3, F32), ("R24", 24, BF), ("SOF", 24, U16),
-       ("ZE", 4224, BF), ("ZA2", 2304, BF), ("ZA3", 2048, BF), ("ZB2", 2048, BF), ("ZB3", 2048, BF), ("ZQ", 2048, BF),
-       ("KG", 768, F32), ("GQ", 256, F32), ("G1U", 768, U16), ("HM", 512, F16), ("QU", 32, U16),
+       ("RL", 96, BF), ("BL", 96, BF), ("OFF", 8, U16), ("CLI", 6, I32), ("CLU", 6, U16), ("XE", 1, F32),
+       ("ZE", 4224, BF), ("ZA", 4352, BF), ("ZB", 4096, BF), ("ZQ", 2048, BF), ("ZOI", 8, I32), ("ZOU", 8, U16),
+       ("KG", 1040, F32), ("GQ", 256, F32), ("G1U", 768, U16), ("HM", 512, F16), ("QU", 32, U16),
        ("G2", 12288, F16), ("X3", 2048, U16), ("G3", 28672, BF),
-       ("REC", 528, BF), ("SA", 528, BF), ("KR", 784, BF), ("KS", 784, BF), ("TQ", 256, BF), ("TS", 256, BF), ("RQ1", 256, BF),
-       ("OWN", 512, BF), ("ZZ", 1152, BF), ("NPG", 1, F32), ("TK2", 1, F32),
+       ("REC", 528, BF), ("SA", 544, BF), ("KR", 1056, BF), ("KS", 1056, BF), ("TQ", 256, BF), ("TS", 256, BF), ("RQ1", 256, BF),
+       ("OWN", 256, BF), ("ZZ", 1152, BF), ("TK2", 1, F32),
        ("SQ0", 528, BF), ("SQ1", 528, BF), ("SQQ", 256, BF), ("DBT", 768, F32), ("SCN", 8192, F32),
-       ("HL", 2, F32), ("UP", 32, F32), ("TT", 32, F32), ("NEW", 32, BF), ("HIT", 32, F32), ("INC", 36, F16), ("YY", 32, F32),
-       ("HD", 32, F32), ("SCF", 16, F32), ("SCU", 16, U16), ("CMF", 32, F32), ("CMU", 32, U16), ("MSG", 48, F16),
+       ("HL", 2, F32), ("UP", 32, F32), ("TT", 32, F32), ("NEW", 32, BF), ("NS", 32, F16), ("INC", 36, F16),
+       ("SCU", 16, U16), ("CMU", 32, U16), ("MSG", 48, F16),
        ("C1", 1, F32), ("NE", 512, BF), ("NC", 2, F32), ("RH", 32, BF), ("MN", 2, F32), ("WS", 256, BF),
        ("PJ", 20, I32), ("PU", 10, U16),
-       ("RKR", 1040, BF), ("RKS", 1040, BF), ("RQ", 256, BF), ("RS", 256, BF), ("RMS", 48, F16), ("RWS", 128, BF),
-       ("RSU", 16, U16), ("FIN", 784, F32), ("YM", 512, F32), ("FL", 768, F32), ("FE", 16, F32)]
+       ("RKR", 528, BF), ("RKS", 1552, BF), ("RQ", 256, BF), ("RS", 256, BF), ("RMS", 48, F16), ("RWS", 128, BF),
+       ("RSU", 16, U16), ("FIN", 1552, F32), ("YM", 512, F32), ("FL", 768, F32), ("FE", 16, F32)]
 SCRATCH = {n: ("sbuf", [128, w], d) for n, w, d in _SB}
 for _b in range(8):
     SCRATCH["PS%d" % _b] = ("psum", [128, 512], F32)
-NCH = 8
-SEMAPHORES = (["cv", "ca", "cp", "cg", "lsem"] + ["d%d" % i for i in range(NCH + 10)] + ["r%d" % i for i in range(8)])
+SEMAPHORES = (["cv", "ca", "cp", "cg", "lsem"] + ["d%d" % i for i in range(24)] + ["r%d" % i for i in range(8)])
 
-CBIG = 201326592.0
-CY = 0.83e-3 * 1.2
-PEC = 0.42e-3 * 1.2
-CG, CS, LAT = 1.56, 3.8, 0.11
+U = 1.0 / 2048
+CHUNKS = (1024, 1024, 1024, 512, 512)
+PA = ((0, 32, 32), (32, 32, 32), (64, 64, 64), (128, 128, 128), (256, 128, 64), (384, 128, 64))
+PB = ((0, 128, 64), (128, 128, 128), (256, 128, 128), (384, 128, 64))
+PC = ((256, 128, 64), (384, 128, 128))
+PD = ((512, 128, 64), (640, 64, 64), (704, 64, 32))
+PE = ((0, 128, 64), (128, 128, 128), (512, 128, 128), (640, 128, 64))
+S2 = 64
+MB = ((0, 1, 3, 4), (0, 1, 3, 4))
 ORDER = """
-20 1 10 0 12 2 3 4 5 6 19 7 28 8 9 13 27 22a 29 15 32 11 33 25 23v 16 38 60 58 36v 24a 14 48 30 53 66 46 67 69 31 68 70 72
-56 35 71 73 90 75 95 92 91 78 76 17 74 54 59 21 55 77 96 99 39 94 106 81 102 100 62 105 101 93 82 84 103 79 87 37 97 104
-111 125 112 107 124 113 108 83 109 131a 110 34 126 88 132 80 137a 89 114 133 115 143 116 47 138 85 127 149a 139 86 144 43
-117 134 128 145 244 155 45 130 146 150 135 245 151 44 140v 156 136 152 129 141 157 118 166 250 142 158 18 41 147 172 167
-148 184a 153 168 119 42 178 120 173 154 246 159 251 40 174 247v 179 49 169 256 50 160v 180 175v 121 181 170 51 185 171v
-186 257 161 176 188v 122 162 177 187 52 252v 182 183 163 189 258 164 248 190v 26 191 63 253 123 199 195 197 263 200 196
-198 192 249v 201 259 207 205 264 203 202 254 208 206 204 209 165 213 266 255v 215 211 210 193 216 217 212 223 214 219 218
-194 221 61 224 265 225 220 260 222 226 295 227 261v 228 231 233 229 232 262v 230 241 296 267 234 236 235 238 237 298 242
-243 301 268v 240 269v 297 270 274 271 302 275 272 304 276 273 277 299 278 321 308 303 280 300v 322 323a 305 281 309 282
-279 310 283 284 324 325 98 314 326 285v 328 327v 331 286 332 287v 329 333 315 306v 288 336 330v 337 294 289 307 334 338
-290 339v 343 335 311 317v 340 341 291 312 358 316 344 313v 368 362 366 369 359 364 346 350 367 365 374 363 376 372 345
-351 375 370 318 373 377 380 319 292 382 371 384 293 320 353 381 342 378 383 388 379 390 352 347 389 385 386 391 348 392
-349 360 387 354 393 361 57 394 239 355 395 400 356 398 64 396 403 65 399 397 404 401 402 406 405 407 357 408 409 410 411
-412 416 413 414 417 418 420 415 419 422 421 428 423 425 429 424v 430 426 427
+1 7 2 3 4 15 0 14 34a 10 9 42 23 22 21 24 62v 54 31 32 20 12 8 13 11 61 37 26 33a 35v 36v 57v 55v 29 60v 58v 28 27 66v
+25 30 56v 19v 38v 59 68 69 67 65 64 70 78 79 82v 91 88 89 71 83 72 84 49 17 16 18 41 48 40 5 6 74 76 87 85 97 90 73 80
+96 109a 115a 81 92 103 98 104 99 121 100 110 105 101 111 93 122a 133a 75 43 116 123 199 117 77 124 112 125 118 134 200
+201 106v 113 135 114v 142 107 108v 205 126 119 136 120 141 206 127v 137v 143 144 86v 146v 202v 138 128 145 210 129 139
+140 130 50 46 51 47 45 39 147 149 211 102v 158 160 154 131 215 159 148v 166 156 207 161 155 162 203 150 168 132 204 151
+167 157 163 94 52 53 44 216 164 174 170 208 169 175 165 218v 172 176 171 177 182 246 173 247 152 178 184 180 212 153
+217 183 209v 181 185 179 95 186 249 252 253 188 63v 189 190 213 191 214v 187 192 193 195v 198 194 219 281 220v 221 197
+225 282 222 226 223 227 228 224 229 248v 254 273a 267a 287 250 251 231 230 232 260 288 233 235 255 236v 234 239 259a
+256v 237 238v 257 261 268 258 262 269 292 274 264v 293 283 240 241 263 270 265 271 266 242 289 275 284v 276v 305 272v
+285 314 310 312 277v 278 286v 315 313 311 279 294 322 320 316 306 317 297 318 324 290 323 298 321 307 291 299 325 319
+328 332 330 329 331 326 295 338 333 327 340 243 341 339 308 336 334 335 337 300 296 301 245 359 244 309 342 358 366 196
+280 304 302 344 343 346 345 347 351 348 349 352 353 354 355 303 350 356 357 363 364 365 360 361 362 369 371 367 368 374
+370v 375v 376 372 373
 """
 
 
@@ -55,7 +58,7 @@ def build(T, topo, core):
     owner = T.cores[(rank + 3) % n_ranks]
     client = T.cores[(rank - 3) % n_ranks]
     ops = []
-    cnt = {"d": 0, "r": 0}
+    cnt = {"d": 0, "r": 0, "w": 0}
 
     def ap(r):
         if r[0] == "ind":
@@ -72,61 +75,50 @@ def build(T, topo, core):
                 out += [r[1], r[2]] if r[0] == "ind" else [r]
         return out
 
-    def num(r):
-        if r[0] == "ind":
-            return 16 * (r[2][2] - r[2][1])
-        st = r[3] if len(r) > 3 else 1
-        return (r[2] - r[1] + st - 1) // st
-
     def sc(x):
         return ap(x) if isinstance(x, tuple) else x
 
-    def add(eng, fn, w, rd, occ, lat=None, kind="c", sem=None, n=1):
+    def add(eng, fn, w, rd, kind="c", sem=None, n=1):
         if w[0] == "ind":
             rd = list(rd) + [w[2]]
             w = w[1]
-        ops.append({"eng": eng, "fn": fn, "w": [w], "r": regs(rd), "occ": occ, "lat": occ if lat is None else lat,
-                    "kind": kind, "sem": sem, "n": n})
-
-    def vcost(o, ins, k):
-        if o[0] == "ind":
-            k = CS
-        elif ins[0][0] == "ind":
-            k = CG
-        return 0.06 + max(64, num(o) * k) * CY
-
-    def half(*rs):
-        return 0.5 if all(r[0] != "ind" and SCRATCH[r[0]][2] in (BF, F16, U16) for r in rs) else 1
+        ops.append({"eng": eng, "fn": fn, "w": [w], "r": regs(rd), "kind": kind, "sem": sem, "n": n})
 
     def ts(o, i, s1, s2, op0, op1=None):
         def fn(q, e):
             if op1 is None:
                 return q.tensor_scalar(ap(o), ap(i), sc(s1), None, op0)
             return q.tensor_scalar(ap(o), ap(i), sc(s1), sc(s2), op0, op1)
-        add("v", fn, o, [i, s1, s2], vcost(o, [i], half(o, i)))
+        add("v", fn, o, [i, s1, s2])
 
     def tt(o, a, b, op):
-        k = 1 if a[0].startswith("PS") or b[0].startswith("PS") else 2
-        add("v", lambda q, e: q.tensor_tensor(ap(o), ap(a), ap(b), op), o, [a, b], vcost(o, [a], k))
+        add("v", lambda q, e: q.tensor_tensor(ap(o), ap(a), ap(b), op), o, [a, b])
 
     def cp(o, i, eng="v"):
         def fn(q, e):
             if e == "v":
                 return q.tensor_copy(ap(o), ap(i))
             return q.activation(ap(o), ap(i), Act.Copy)
-        add(eng, fn, o, [i], vcost(o, [i], half(o, i) if eng == "v" else 1))
+        add(eng, fn, o, [i])
 
-    def act(o, i, func=Act.Identity, bias=0.0, scale=1.0):
-        add("a", lambda q, e: q.activation(ap(o), ap(i), func, bias=sc(bias), scale=sc(scale)), o, [i, bias, scale], vcost(o, [i], 1))
+    def lin(o, i, scale, bias, eng="av"):
+        def fn(q, e):
+            if e == "v":
+                return q.tensor_scalar(ap(o), ap(i), sc(scale), sc(bias), Alu.mult, Alu.add)
+            return q.activation(ap(o), ap(i), Act.Identity, bias=sc(bias), scale=sc(scale))
+        add(eng, fn, o, [i, scale, bias])
+
+    def square(o, i):
+        add("a", lambda q, e: q.activation(ap(o), ap(i), Act.Square, scale=0.70710678), o, [i])
 
     def ms(o, v):
-        add("v", lambda q, e: q.memset(ap(o), v), o, [], vcost(o, [o], half(o)))
+        add("v", lambda q, e: q.memset(ap(o), v), o, [])
 
     def red(o, i, op, neg=False):
-        add("v", lambda q, e: q.tensor_reduce(ap(o), ap(i), Ax.X, op, negate=neg), o, [i], 0.06 + max(64, num(i)) * CY)
+        add("v", lambda q, e: q.tensor_reduce(ap(o), ap(i), Ax.X, op, negate=neg), o, [i])
 
     def scan(o, d0, d1, init, op0, op1):
-        add("v", lambda q, e: q.tensor_tensor_scan(ap(o), ap(d0), ap(d1), sc(init), op0, op1), o, [d0, d1, init], vcost(o, [d0], 1))
+        add("v", lambda q, e: q.tensor_tensor_scan(ap(o), ap(d0), ap(d1), sc(init), op0, op1), o, [d0, d1, init])
 
     def mm(items):
         def fn(q, e):
@@ -137,8 +129,7 @@ def build(T, topo, core):
         rd = []
         for it in items:
             rd += [it[1], it[2]]
-        c = sum(max(64, num(it[2])) for it in items) * PEC
-        add("p", fn, items[0][0], rd, c, c + 0.05)
+        add("p", fn, items[0][0], rd)
 
     def acc(o, prs):
         mm([(o, l, r, i == 0, i == len(prs) - 1) for i, (l, r) in enumerate(prs)])
@@ -148,40 +139,41 @@ def build(T, topo, core):
             if SCRATCH[o[0]][2] == I32:
                 return q.iota(ap(o), pat, base, cm)
             return q.iota(ap(o), pat, base, cm, allow_small_or_imprecise_dtypes=True)
-        add("g", fn, o, [], 0.13 + 2 * num(o) * CY)
+        add("g", fn, o, [])
 
     def pick(o, i, pat, op, cm):
-        add("g", lambda q, e: q.affine_select(ap(o), ap(i), pat, op, 0.0, 0, cm), o, [i], 0.17 + 256 * CY)
+        add("g", lambda q, e: q.affine_select(ap(o), ap(i), pat, op, 0.0, 0, cm), o, [i])
 
-    def fill1(o):
+    def fill1(o, v):
+        n = o[2] - o[1]
+
         def fn(q, e):
             if e == "v":
-                return q.memset(ap(o), 0.0)
+                return q.memset(ap(o), float(v))
             if e == "a":
-                return q.activation(ap(o), T.ZZ[:, 0:num(o)], Act.Copy)
-            return q.iota(ap(o), [[0, num(o)]], 0, 0, allow_small_or_imprecise_dtypes=True)
-        add("gav", fn, o, [("ZZ", 0, 1152)], 0.13 + 2 * num(o) * CY)
-        ops[-1]["alt"] = {"v": 0.06 + 0.5 * num(o) * CY, "a": 0.07 + num(o) * CY}
+                return q.activation(ap(o), T.ZZ[:, 0:n], Act.Identity, bias=float(v))
+            return q.iota(ap(o), [[0, n]], v, 0, allow_small_or_imprecise_dtypes=True)
+        add("gav", fn, o, [("ZZ", 0, 1152)])
 
-    def fill(name, lo, hi):
+    def fill(name, lo, hi, v=0):
         for a in range(lo, hi, 1152):
-            fill1((name, a, min(hi, a + 1152)))
+            fill1((name, a, min(hi, a + 1152)), v)
 
-    def dma(eng, prs, w, rd, lat):
+    def dma(eng, prs, w, rd):
         s = "d%d" % cnt["d"]
         cnt["d"] += 1
 
         def fn(q, e):
             for o, i in prs:
                 q.dma_start(o, i).then_inc(T.sem[s], 16)
-        add(eng, fn, w, rd, 0.07 * len(prs), lat, "d", s, 16 * len(prs))
+        add(eng, fn, w, rd, "d", s, 16 * len(prs))
 
-    def send(dst, o, i, lat):
+    def send(dst, o, i):
         s = "r%d" % cnt["r"]
         cnt["r"] += 1
         rid, pid, _ = topo.addr(dst)
         add("g", lambda q, e: q.remote_dma(ap(o), ap(i), T.sem[s], T.sem.lsem, pid, rid, topo.mask(core, dst)),
-            o, [i], 0.4, lat, "r", s, len(topo.engines(core, dst)))
+            o, [i], "r", s, len(topo.engines(core, dst)))
 
     def ind(w, o):
         return ("ind", w, o)
@@ -192,109 +184,93 @@ def build(T, topo, core):
     def dd(i):
         return ("DB", 15 - i, 143 - i)
 
-    PI, PG = ("PCF", 0, 1), ("PCF", 1, 2)
+    PI, PG, PP = ("PCF", 0, 1), ("PCF", 1, 2), ("PCF", 2, 3)
     E16 = ("M16", 0, 16)
+    IDN, BO = ("IDN", 0, 128), ("BO", 0, 128)
 
-    dma("a", [(T.SIN[:, 0:16], T.bk[:, :]), (T.SIN[:, 16:48], T.qc[:, :]), (T.SIN[:, 48:80], T.qs[:, :])], ("SIN", 0, 80), [], 2.2)
-    dma("s", [(T.SIN[:, 80:83], T.ex[:, :]), (T.SIN[:, 83:89], T.zs[:, :])], ("SIN", 80, 89), [], 2.2)
-    cw = 4096 // NCH
-    for c in range(NCH):
-        dma("s", [(T.MT[:, c * cw:(c + 1) * cw], T.mt[:, c * cw:(c + 1) * cw])], ("MT", c * cw, (c + 1) * cw), [], 2.3 + (c + 1) * 7.0 / NCH)
-        ops[-1]["after"] = len(ops) - 2
-    iota(("IPI", 0, 1), [[0, 1]], 0, 1)
-    iota(("ICF", 0, 128), [[1, 128]], 0, 0)
+    dma("a", [(T.SIN[:, 0:16], T.bk[:, :]), (T.SIN[:, 16:48], T.qc[:, :]), (T.SIN[:, 48:80], T.qs[:, :])], ("SIN", 0, 80), [])
+    dma("s", [(T.SIN[:, 80:83], T.ex[:, :]), (T.SIN[:, 83:89], T.zs[:, :])], ("SIN", 80, 89), [])
+    cuts = [sum(CHUNKS[:c]) for c in range(len(CHUNKS) + 1)]
+    for lo, hi in zip(cuts, cuts[1:]):
+        dma("s", [(T.MT[:, lo:hi], T.mt[:, lo:hi])], ("MT", lo, hi), [])
+    iota(("PCI", 2, 3), [[0, 1]], 0, 1)
+    iota(("CLI", 0, 6), [[3, 3], [1, 2]], 1, 0)
     iota(("G16", 0, 128), [[16, 8], [0, 16]], 0, 0)
     iota(("C16", 0, 128), [[0, 8], [1, 16]], 0, 0)
-    send(owner, ("LIN", 0, 89), ("SIN", 0, 89), 4.0)
+    send(owner, ("LIN", 0, 89), ("SIN", 0, 89))
     iota(("PRI", 0, 128), [[0, 128]], 1, 0)
-    pick(("IDN", 0, 128), ("PRI", 0, 128), [[-1, 128]], Alu.is_equal, 1)
-    pick(("PRM", 0, 128), ("PRI", 0, 128), [[-1, 16], [-16, 8]], Alu.is_equal, 1)
-    iota(("ZOI", 0, 16), [[128, 16]], 0, 1)
+    pick(IDN, ("PRI", 0, 128), [[-1, 128]], Alu.is_equal, 1)
     iota(("J16", 0, 16), [[16, 16]], 0, 0)
     ms(("ZZ", 0, 1152), 0.0)
     fill("ZE", 0, 4224)
     ms(("DB", 0, 144), 0.0)
-    ms(("INC", 0, 1), 16.0)
-    ts(("PCI", 0, 1), ("IPI", 0, 1), 15, None, Alu.bitwise_and)
-    ts(("PCI", 1, 2), ("IPI", 0, 1), 112, None, Alu.bitwise_and)
-    cp(("PCF", 0, 2), ("PCI", 0, 2))
-    act(("NPG", 0, 1), PG, scale=-1.0)
-    act(("IC16", 0, 128), ("ICF", 0, 128), bias=("NPG", 0, 1))
-    ts(("BO", 0, 128), ("G16", 0, 128), PG, None, Alu.is_equal)
+    ms(("INC", 0, 1), 16.0 * U)
+    ts(("PCI", 0, 1), ("PCI", 2, 3), 15, None, Alu.bitwise_and)
+    ts(("PCI", 1, 2), ("PCI", 2, 3), 112, None, Alu.bitwise_and)
+    cp(("PCF", 0, 3), ("PCI", 0, 3))
+    cp(("CLU", 0, 6), ("CLI", 0, 6))
+    lin(("XE", 0, 1), PI, 128.0, PG)
+    for s, o in enumerate((2176.0, 2304.0, 2048.0)):
+        ts(("OFF", 2 * s + 1, 2 * s + 2), ("XE", 0, 1), o, None, Alu.add)
+    cp(("OFF", 6, 7), PP)
+    ts(BO, ("G16", 0, 128), PG, None, Alu.is_equal)
     ts(("M16", 0, 128), ("C16", 0, 128), PI, None, Alu.is_equal)
-    fill("ZA2", 0, 2304)
-    fill("ZA3", 0, 2048)
-    cp(("DB", 15, 143, 16), ("BO", 0, 128, 16), "a")
-    act(("BON", 0, 128), ("BO", 0, 128), scale=-1.0)
-    pick(("TRI", 0, 128), ("BO", 0, 128), [[1, 128]], Alu.is_gt, -1)
-    fill("ZQ", 0, 2048)
-    iota(("KG", 256, 768), [[0, 512]], 0, 0)
-    fill("ZB2", 0, 2048)
-    fill("ZB3", 0, 2048)
-    iota(("KR", 272, 784), [[0, 512]], -1, 0)
-    iota(("KS", 272, 784), [[0, 512]], -1, 0)
-    iota(("RKR", 528, 1040), [[0, 512]], -1, 0)
-    iota(("RKS", 528, 1040), [[0, 512]], -1, 0)
-    cp(("ZOU", 0, 16), ("ZOI", 0, 16))
-    act(("NN", 0, 16), ("J16", 0, 16), bias=PI)
-    act(("CB", 0, 16), ("NN", 0, 16), bias=256.0, scale=1.0 / 512)
-    for k in range(3):
-        act(("SL", 16 * k, 16 * k + 16), ("NN", 0, 16), bias=256.0 * (k + 1))
-    act(("TK", 0, 1), PI, bias=1000.0, scale=1.0 / 8192)
-    act(("EF", 0, 2), ("M16", 0, 2), bias=1.0, scale=-1.0)
-    act(("TK2", 0, 1), PI, scale=1.0 / 8192)
-    act(("TBC", 0, 16), E16, scale=("TK2", 0, 1))
+    fill("ZA", 0, 4352)
+    cp(("DB", 15, 143, 16), ("BO", 0, 128, 16), "av")
+    lin(("BON", 0, 128), BO, -1.0, 0.0)
+    pick(("TRI", 0, 128), BO, [[1, 128]], Alu.is_gt, -1)
+    fill1(("ZQ", 0, 1024), 0)
+    fill1(("ZQ", 1024, 2048), 0)
+    iota(("ZOI", 0, 8), [[128, 8]], 0, 1)
+    cp(("ZOU", 0, 8), ("ZOI", 0, 8))
+    fill("KG", 256, 1040)
+    fill("ZB", 0, 4096)
+    fill("SA", 272, 288, -1)
+    fill("KR", 272, 1056, -1)
+    fill("KS", 272, 1056, -1)
+    fill("FIN", 528, 1552, -1)
+    fill("RKS", 528, 1552, -1)
+    lin(("NN", 0, 16), ("J16", 0, 16), 1.0, PI)
+    lin(("CB", 0, 16), ("NN", 0, 16), 1.0 / 512, 256.0)
+    for t, top in ((0, 272.0), (1, 512.0)):
+        lin(("SLN", 16 * t, 16 * t + 16), ("NN", 0, 16), -1.0, -top)
+        lin(("SLU", 16 * t, 16 * t + 16), ("NN", 0, 16), U, top * U)
+    lin(("TK", 0, 1), PI, 1.0 / 8192, 1000.0)
+    lin(("EF", 0, 2), ("M16", 0, 2), -1.0, 1.0)
+    lin(("TK2", 0, 1), PI, 1.0 / 8192, 0.0)
+    lin(("TBC", 0, 16), E16, ("TK2", 0, 1), 0.0)
     for t in range(2):
-        act(("KC", 128 * t, 128 * t + 128), dd(t), bias=-1000.0, scale=("TK", 0, 1))
-        act(("IM", 128 * t, 128 * t + 128), ("IDN", 0, 128), scale=("EF", t, t + 1))
+        lin(("KC", 128 * t, 128 * t + 128), dd(t), ("TK", 0, 1), -1000.0)
+        lin(("IM", 128 * t, 128 * t + 128), IDN, ("EF", t, t + 1), 0.0)
 
-    for c in range(NCH):
-        lo, hi = c * cw, (c + 1) * cw
-        ts(("NX", lo, hi), ("MT", lo, hi), -7.5, CBIG, Alu.add, Alu.add)
-        act(ps(c % 2, 0, cw), ("NX", lo, hi), bias=-CBIG)
-        tt(("OT", lo, hi), ("MT", lo, hi), ps(c % 2, 0, cw), Alu.subtract)
+    for lo, hi in zip(cuts, cuts[1:]):
+        lin(("NX", lo, hi), ("MT", lo, hi), 0.0625, -0.46875)
+        ts(("MT", lo, hi), ("MT", lo, hi), 15, None, Alu.bitwise_and)
 
     cp(("LU", 0, 48), ("LIN", 0, 48))
     cp(("WF", 0, 25), ("LIN", 64, 89))
     ts(("KI", 0, 16), ("LIN", 48, 64), 6, None, Alu.arith_shift_right)
     cp(("KU", 0, 16), ("KI", 0, 16))
-    act(("W0", 0, 3), ("WF", 16, 25, 3), bias=PG, scale=128.0)
-    cp(("MSK", 0, 512), ind(E16, ("LU", 16, 48)), "a")
-    act(("SP", 0, 16), ("WF", 0, 16), scale=1.0 / 16384)
-    cp(("REC", 0, 16), ("WF", 3, 19), "a")
-    cp(("SA", 0, 16), ("WF", 6, 22), "a")
-    cp(("KS", 0, 16), ("WF", 9, 25), "a")
+    cp(("MSK", 0, 256), ind(E16, ("LU", 16, 32)), "av")
+    cp(("MSK", 256, 512), ind(E16, ("LU", 32, 48)), "av")
+    lin(("SP", 0, 16), ("WF", 0, 16), 0.125, 0.0)
+    cp(("REC", 0, 16), ("WF", 3, 19), "av")
+    cp(("SA", 0, 16), ("WF", 6, 22), "av")
+    cp(("KS", 0, 16), ("WF", 9, 25), "av")
+    ZS = (("ZE", 2176, 4224), ("ZA", 2304, 4352), ("ZB", 2048, 4096))
+    tt(("RL", 0, 96), ind(("WF", 16, 25), ("CLU", 0, 6)), ("M16", 0, 96), Alu.mult)
+    acc(ps(2, 256, 352), [(BO, ("RL", 0, 96))])
+    ts(("BL", 0, 96), ps(2, 256, 352), PI, None, Alu.is_equal)
+    ts(("OFF", 0, 6, 2), ("WF", 16, 25, 3), 128.0, PP, Alu.mult, Alu.add)
     for s in range(3):
-        act(("R24", 8 * s, 8 * s + 8), ("BO", 0, 128, 16), scale=("W0", s, s + 1))
-    acc(ps(2, 256, 280), [(("M16", 0, 128), ("R24", 0, 24))])
-    ts(("SOF", 0, 24), ps(2, 256, 280), PI, None, Alu.add)
-    Z2 = [("ZE", 0), ("ZA2", 0), ("ZB2", 0)]
-    Z3 = [("ZE", 2176), ("ZA3", 0), ("ZB3", 0)]
-
-    def selectors(s, b):
-        p2, p3 = ("PT", 256 * s, 256 * s + 128), ("PT", 256 * s + 128, 256 * s + 256)
-        ts(p2, ("IC16", 0, 128), ("WF", 17 + 3 * s, 18 + 3 * s), None, Alu.is_equal)
-        ts(p3, ("IC16", 0, 128), ("WF", 18 + 3 * s, 19 + 3 * s), None, Alu.is_equal)
-        it = [(ps(b, 0, 128), p2, ("IDN", 0, 128), True, True), (ps(b, 128, 256), p3, ("PRM", 0, 128), True, True)]
-        if s == 1:
-            it.append((ps(b, 256, 384), p3, ("IDN", 0, 128), True, True))
-        mm(it)
-        cp(("P2C", 128 * s, 128 * s + 128), ps(b, 0, 128), "a")
-        cp((Z3[s][0], Z3[s][1], Z3[s][1] + 2048, 16), ps(b, 128, 256), "a")
-        if s == 1:
-            cp(("ZA2", 2176, 2304), ps(b, 256, 384), "a")
-        cp(ind((Z2[s][0], 0, 2048), ("SOF", 8 * s, 8 * s + 8)), ("P2C", 128 * s, 128 * s + 128))
-
-    selectors(0, 2)
-    selectors(1, 7)
-    selectors(2, 7)
-    WNX, WOT = ("NX", 0, 4096), ("OT", 0, 4096)
-    CENTRE = -(CBIG / 16 + 2048.0)
+        cp(ind((ZS[s][0], 0, ZS[s][2]), ("OFF", 2 * s, 2 * s + 2)), ("BL", 32 * s, 32 * s + 32))
+    cp(ind(("ZA", 2176, 2304), ("OFF", 6, 7)), ("BL", 48, 64))
+    WNX, WOT = ("NX", 0, 4096), ("MT", 0, 4096)
 
     def step1(lst, k0, keep):
-        ts(("G1U", k0, k0 + 256), ind(WNX, lst), CBIG, 1.0 / 16, Alu.subtract, Alu.mult)
+        cp(("G1U", k0, k0 + 256), ind(WNX, lst))
         if keep is not None:
-            act(keep, ind(WNX, lst), bias=CENTRE, scale=1.0 / 16)
+            lin(keep, ind(WNX, lst), 1.0, -2048.0)
 
     def queries(t):
         tt(("HM", 256 * t, 256 * t + 256), ind(("KG", 0, 256 * (t + 1)), ("KU", 16 * t, 16 * t + 16)), ("MSK", 256 * t, 256 * t + 256), Alu.mult)
@@ -303,151 +279,142 @@ def build(T, topo, core):
         step1(("QU", 16 * t, 16 * t + 16), 256 * (t + 1), ("GQ", 0, 256) if t == 0 else None)
 
     def step2(k0, w):
-        o, i = ("G2", 16 * k0, 16 * (k0 + w)), ind(WNX, ("G1U", k0, k0 + w))
-
-        def fn(q, e):
-            if e == "v":
-                return q.tensor_scalar(ap(o), ap(i), CBIG + 32768.0, 1.0 / 16, Alu.subtract, Alu.mult)
-            return q.activation(ap(o), ap(i), Act.Identity, bias=CENTRE, scale=1.0 / 16)
-        add("va", fn, o, [i], vcost(o, [i], 1))
+        for u in range(k0, k0 + w, S2):
+            v = min(u + S2, k0 + w)
+            lin(("G2", 16 * u, 16 * v), ind(WNX, ("G1U", u, v)), 1.0, -2048.0, "va")
 
     def dest(s, k):
         if s == 0:
             return ("REC", 16 + k) if k < 512 else ("RQ1", k - 512)
         if s == 1:
-            return ("SA", 16 + k)
-        return ("KS", 16 + k) if k < 256 or k >= 512 else ("TS", k - 256)
+            return ("SA", 16 + k if k < 256 else 32 + k)
+        return (("KS", 16 + k), ("TS", k - 256), ("OWN", k - 512))[k // 256]
 
     def walk(s, k0, w, sub):
-        b2, b3 = (3, 4) if s == 0 else (5, 6)
+        b2, b3 = ((3, 4), (0, 1))[cnt["w"] % 2] if s == 0 else (5, 6)
+        cnt["w"] += s == 0
         x0 = (0, 768, 1280)[s] + k0
         y0 = (k0 % 512, 512 + k0, 1024 + k0)[s]
-        z, o = Z2[s]
-        acc(ps(b2, 0, w), [((z, 128 * a, 128 * a + 128), ("G2", 16 * k0 + a, 16 * (k0 + w), 16)) for a in range(16)])
+        acc(ps(b2, 0, w), [((ZS[s][0], 128 * a, 128 * a + 128), ("G2", 16 * k0 + a, 16 * (k0 + w), 16)) for a in range(16)])
         ts(("X3", x0, x0 + w), ps(b2, 0, w), 2048.0, None, Alu.add)
         for u in range(0, w, sub):
             cp(("G3", 16 * (y0 + u), 16 * (y0 + u + sub)), ind(WOT, ("X3", x0 + u, x0 + u + sub)), "av")
-        z, o = Z3[s]
+        z, o = ZS[s][:2]
         acc(ps(b3, 0, w), [((z, o + 127 * e, o + 127 * e + 128), ("G3", 16 * y0 + e, 16 * (y0 + w), 16)) for e in range(16)])
         d, c0 = dest(s, k0)
         cp((d, c0, c0 + w), ps(b3, 0, w), "av")
-        if s and k0 >= 256 * s:
-            cp(("OWN", k0 - 256, k0 - 256 + w), ps(b3, 0, w), "av")
-
-    RT = 0.70710678
 
     def known_side(t, src, sq):
         n = 256 * (t + 1)
-        act((sq, 15, 16 + n), (src, 15, 16 + n), Act.Square, scale=RT)
-        acc(ps(7, 0, n), [(("BO", 0, 128), (sq, 16, 16 + n)), (("BON", 0, 128), (sq, 15, 15 + n))])
-        act(("DBT", 256 * t, 256 * t + n), ps(7, 0, n), bias=1.0 / 2048)
-        acc(ps(7, 0, 2), [(("BO", 0, 128), (sq, 14 + n, 16 + n))])
-        act(("HL", t, t + 1), ps(7, 1, 2), bias=(n - 1) / 2048.0)
+        square((sq, 15, 16 + n), (src, 15, 16 + n))
+        acc(ps(7, 0, n), [(BO, (sq, 16, 16 + n)), (("BON", 0, 128), (sq, 15, 15 + n))])
+        lin(("DBT", 256 * t, 256 * t + n), ps(7, 0, n), 1.0, U)
+        acc(ps(7, 0, 2), [(BO, (sq, 14 + n, 16 + n))])
+        lin(("HL", t, t + 1), ps(7, 1, 2), 1.0, (n - 1) * U)
+
+    def spread(rq, lo, hi):
+        cp(ind(("ZQ", 8 * lo, 8 * hi), ("ZOU", 0, 8)), (rq[0], rq[1] + lo, rq[1] + hi))
 
     def match(t, rq, sq, known):
         n = 256 * (t + 1)
         c = (16 * t, 16 * t + 16)
-        cp(ind(("ZQ", 0, 2048), ("ZOU", 0, 16)), rq)
-        act(sq, rq, Act.Square, scale=RT)
+        spread(rq, 0, 128)
+        spread(rq, 128, 256)
+        square(sq, rq)
         acc(ps(2, 0, 16), [(dd(i), (sq[0], sq[1] + i, sq[2], 16)) for i in range(16)])
-        act(("UP",) + c, ps(2, 0, 16), bias=("HL", t, t + 1))
+        lin(("UP",) + c, ps(2, 0, 16), 1.0, ("HL", t, t + 1))
         for j in range(16):
-            b = (0, 1, 3, 4)[j % 4]
+            b = MB[t][j % len(MB[t])]
             acc(ps(b, 0, n), [(("ZQ", 128 * j, 128 * j + 128), (known, 16, 16 + n))])
             scan(("SCN", 512 * j, 512 * j + n), ("DBT", 256 * t, 256 * t + n), ps(b, 0, n), -1.0e9, Alu.add, Alu.max)
         tt(("TT",) + c, ("UP",) + c, ("SCN", n - 1, 8192, 512), Alu.subtract)
-        ts(("NEW",) + c, ("TT",) + c, 0.4, None, Alu.is_ge)
+        ts(("CMU",) + c, ("TT",) + c, 2048.0, float(n), Alu.mult, Alu.min)
+        ts(("NEW",) + c, ("TT",) + c, 0.4, U, Alu.is_ge, Alu.mult)
         i0 = 18 * t
-        scan(("INC", i0 + 1, i0 + 17), ("NEW",) + c, ("NEW",) + c, 16.0 if t == 0 else ("C1", 0, 1), Alu.add, Alu.max)
-        mm([(ps(2, 0, 17), ("BO", 0, 128), ("INC", i0, i0 + 17), True, False), (ps(2, 0, 16), ("TRI", 0, 128), ("NEW",) + c, False, True)])
-        ts(("HIT",) + c, ("TT",) + c, 0.4, None, Alu.is_lt)
-        tt(("HD",) + c, ("HIT",) + c, ("SL", 16 * (t + 1), 16 * (t + 2)), Alu.mult)
-        ts(("YY",) + c, ("TT",) + c, 2048.0, None, Alu.mult)
+        scan(("INC", i0 + 1, i0 + 17), ("NEW",) + c, ("NEW",) + c, 16.0 * U if t == 0 else ("C1", 0, 1), Alu.add, Alu.max)
+        tt(("NS",) + c, ("NEW",) + c, ("SLN",) + c, Alu.mult)
+        p = ps(2, 0, 16)
+        mm([(ps(2, 0, 17), BO, ("INC", i0, i0 + 17), True, False), (p, IDN, ("SLU",) + c, False, False),
+            (p, ("TRI", 0, 128), ("NEW",) + c, False, False), (p, IDN, ("NS",) + c, False, True)])
         if t == 0:
-            tt(("SCF", 0, 16), ("HD",) + c, ps(2, 0, 16), Alu.max)
-            cp(("SCU", 0, 16), ("SCF", 0, 16))
+            ts(("SCU", 0, 16), p, 2048.0, -256.0, Alu.mult, Alu.add)
             ts(("KI", 16, 32), ("SP", 0, 16), ps(2, 16, 17), -0.499969482421875, Alu.mult, Alu.add)
             cp(("KU", 16, 32), ("KI", 16, 32))
-            act(("C1", 0, 1), ps(2, 16, 17), scale=1.0 / 16)
-            cp(("INC", 18, 19), ("C1", 0, 1))
+            lin(("C1", 0, 1), ps(2, 16, 17), 1.0 / 16, 0.0)
+            cp(("INC", 18, 19), ("C1", 0, 1), "av")
         else:
-            tt(("MSG", 32, 48), ("HD",) + c, ps(2, 0, 16), Alu.max)
-        tt(("MSG",) + c, ("YY",) + c, ps(2, 0, 16), Alu.min)
-        tt(("CMF",) + c, ("YY",) + c, ("SL",) + c, Alu.min)
-        cp(("CMU",) + c, ("CMF",) + c)
+            cp(("MSG", 32, 48), p, "va")
+        tt(("MSG",) + c, ("TT",) + c, p, Alu.min)
 
-    def winner(t, src):
+    def winner(t, src, own):
         n = 256 * (t + 1)
         ne = ("NE", 256 * t, 256 * t + 256)
-        tt(ne, ind((src, 16, 272 + n), ("CMU", 16 * t, 16 * t + 16)), ("OWN", n - 256, n), Alu.not_equal)
+        tt(ne, ind((src, 16, 32 + n), ("CMU", 16 * t, 16 * t + 16)), own, Alu.not_equal)
         red(("NC", t, t + 1), ne, Alu.add, True)
-        ts(("RH", 16 * t, 16 * t + 16), E16, ("NC", t, t + 1), None, Alu.mult)
-        acc(ps(2, 0, 16), [(("BO", 0, 128), ("RH", 16 * t, 16 * t + 16)), (("BO", 0, 128), ("TBC", 0, 16))])
-        red(("MN", t, t + 1), ps(2, 0, 16), Alu.min)
+        lin(("RH", 16 * t, 16 * t + 16), E16, ("NC", t, t + 1), 0.0, "va")
+        acc(ps(7, 0, 16), [(BO, ("RH", 16 * t, 16 * t + 16)), (BO, ("TBC", 0, 16))])
+        red(("MN", t, t + 1), ps(7, 0, 16), Alu.min)
         ts(("WS", 128 * t, 128 * t + 128), ("KC", 128 * t, 128 * t + 128), ("NC", t, t + 1), ("MN", t, t + 1), Alu.add, Alu.is_equal)
 
     step1(("LU", 0, 16), 0, ("KG", 0, 256))
     queries(0)
-    for k0, w, sub in ((0, 32, 32), (32, 32, 32), (64, 64, 64), (128, 64, 64), (192, 64, 64), (256, 64, 64), (320, 64, 64),
-                       (384, 64, 64), (448, 64, 32)):
+    for k0, w, sub in PA:
         step2(k0, w)
         walk(0, k0, w, sub)
-        if k0 == 192:
+        if k0 + w == 256:
             known_side(0, "REC", "SQ0")
     match(0, ("REC", 272, 528), ("SQ0", 272, 528), "REC")
-    cp(ind(("KG", 0, 768), ("SCU", 0, 16)), ("GQ", 0, 256))
-    for k0 in range(0, 512, 128):
-        walk(1, k0, 128, 64)
+    cp(ind(("KG", 256, 1040), ("SCU", 0, 16)), ("GQ", 0, 256))
+    for x in PB:
+        walk(1, *x)
     queries(1)
-    winner(0, "SA")
+    winner(0, "SA", ("SA", 288, 544))
     ts(("PJ", 0, 9), ("CB", 0, 9), ("MN", 0, 1), 8192.0, Alu.add, Alu.mult)
     ts(("PJ", 10, 19), ("PJ", 0, 9), 8191, None, Alu.bitwise_and)
     cp(("PU", 0, 9), ("PJ", 10, 19))
-    cp(("ZE", 0, 2304, 16), ind(("ZA2", 0, 2304), ("PU", 0, 9)))
-    acc(ps(7, 0, 256), [(("IM", 0, 128), ("REC", 272, 528)), (("WS", 0, 128), ("SA", 272, 528))])
+    cp(("ZE", 0, 2304, 16), ind(("ZA", 0, 2304), ("PU", 0, 9)), "va")
+    acc(ps(7, 0, 256), [(("IM", 0, 128), ("REC", 272, 528)), (("WS", 0, 128), ("SA", 288, 544))])
     cp(("TQ", 0, 256), ps(7, 0, 256), "av")
     acc(ps(7, 0, 272), [(("IM", 0, 128), ("REC", 0, 272)), (("WS", 0, 128), ("SA", 0, 272))])
     cp(("KR", 0, 272), ps(7, 0, 272), "av")
-    cp(ind(("KR", 16, 784), ("SCU", 0, 16)), ("TQ", 0, 256))
+    cp(ind(("KR", 272, 1056), ("SCU", 0, 16)), ("TQ", 0, 256))
     known_side(1, "KR", "SQ1")
-    send(client, ("RKR", 0, 528), ("KR", 0, 528), 4.5)
-    walk(2, 256, 128, 64)
-    walk(2, 384, 128, 64)
-    cp(ind(("KS", 16, 784), ("SCU", 0, 16)), ("TS", 0, 256))
-    walk(2, 0, 128, 64)
-    walk(2, 128, 128, 64)
-    send(client, ("RKS", 0, 528), ("KS", 0, 528), 4.5)
-    for k0 in range(512, 768, 64):
-        step2(k0, 64)
-    walk(0, 512, 128, 64)
-    walk(0, 640, 64, 64)
-    walk(0, 704, 64, 32)
-    send(client, ("RQ", 0, 256), ("RQ1", 0, 256), 3.5)
-    walk(2, 512, 128, 64)
-    walk(2, 640, 128, 64)
-    send(client, ("RS", 0, 256), ("OWN", 256, 512), 3.5)
+    send(client, ("RKR", 0, 528), ("KR", 0, 528))
+    for x in PC:
+        walk(2, *x)
+    cp(ind(("KS", 272, 1056), ("SCU", 0, 16)), ("TS", 0, 256))
+    send(client, ("RKS", 272, 528), ("KS", 272, 528))
+    for k0, w, sub in PD:
+        step2(k0, w)
+        walk(0, k0, w, sub)
+    send(client, ("RQ", 0, 256), ("RQ1", 0, 256))
+    for x in PE:
+        walk(2, *x)
+    send(client, ("RS", 0, 256), ("OWN", 0, 256))
+    send(client, ("RKS", 0, 272), ("KS", 0, 272))
     match(1, ("RQ1", 0, 256), ("SQQ", 0, 256), "KR")
-    send(client, ("RMS", 0, 48), ("MSG", 0, 48), 2.5)
-    winner(1, "KS")
-    send(client, ("RWS", 0, 128), ("WS", 128, 256), 2.7)
-    cp(("RSU", 0, 16), ("RMS", 32, 48))
-    cp(ind(("RKR", 16, 1040), ("RSU", 0, 16)), ("RQ", 0, 256))
-    cp(ind(("RKS", 16, 1040), ("RSU", 0, 16)), ("RS", 0, 256))
+    send(client, ("RMS", 0, 48), ("MSG", 0, 48))
+    winner(1, "KS", ("OWN", 0, 256))
+    send(client, ("RWS", 0, 128), ("WS", 128, 256))
+    cp(("FIN", 16, 272), ("RKR", 16, 272), "av")
+    cp(("FIN", 272, 528), ("RKR", 272, 528), "av")
+    ts(("RSU", 0, 16), ("RMS", 32, 48), 2048.0, -256.0, Alu.mult, Alu.add)
+    cp(ind(("RKS", 272, 1552), ("RSU", 0, 16)), ("RS", 0, 256))
+    cp(ind(("FIN", 272, 1552), ("RSU", 0, 16)), ("RQ", 0, 256))
     mm([(ps(7, i, 512, 16, 8), ("IDN", i, 128, 16), ("RMS", 0, 32), True, True) for i in range(16)])
-    cp(("YM", 0, 512, 1, 8), ps(7, 0, 512, 1, 8), "a")
-    dma("s", [(T.ym[:, :], T.YM[0:8, :])], ("ym", 0, 512), [("YM", 0, 512)], 2.2)
-    cp(("FIN", 16, 400), ("RKR", 16, 400), "av")
-    cp(("FIN", 400, 784), ("RKR", 400, 784), "av")
+    lin(("YM", 0, 512, 1, 8), ps(7, 0, 512, 1, 8), 2048.0, 0.0)
+    dma("s", [(T.ym[:, :], T.YM[0:8, :])], ("ym", 0, 512), [("YM", 0, 512)])
     rows = [(0, 1)] + [(16 * k + 2, min(16 * k + 17, 128)) for k in range(8)]
+    dma("s", [(T.yr[a:b, 0:256], T.FIN[a:b, 16:272]) for a, b in rows], ("yr0", 0, 1), [("FIN", 16, 272)])
     for q, part in (("s", rows[:5]), ("a", rows[5:])):
-        dma(q, [(T.yr[a:b, :], T.FIN[a:b, 16:784]) for a, b in part], ("yr" + q, 0, 1), [("FIN", 16, 784)], 3.2)
+        dma(q, [(T.yr[a:b, 256:768], T.FIN[a:b, 272:784]) for a, b in part], ("yr" + q, 0, 1), [("FIN", 272, 784)])
     for b, lo in ((3, 0), (4, 384)):
         acc(ps(b, 0, 384, 1, 8), [(("RWS", 1, 128, 16), ("RKS", 16 + lo, 400 + lo))])
         cp(("FL", lo, lo + 384, 1, 8), ps(b, 0, 384, 1, 8), "av")
-    dma("s", [(T.yr[1:128:16, :], T.FL[0:8, :])], ("yr1", 0, 1), [("FL", 0, 768)], 2.2)
+    dma("s", [(T.yr[1:128:16, :], T.FL[0:8, :])], ("yr1", 0, 1), [("FL", 0, 768)])
     acc(ps(2, 0, 16), [(("IM", 128, 256), ("RKR", 0, 16)), (("RWS", 0, 128), ("RKS", 0, 16))])
     cp(("FE", 0, 16), ps(2, 0, 16), "av")
-    dma("s", [(T.ye[:, :], T.FE[:, 13:16])], ("ye", 0, 1), [("FE", 0, 16)], 2.2)
+    dma("s", [(T.ye[:, :], T.FE[:, 13:16])], ("ye", 0, 1), [("FE", 0, 16)])
     return ops
 
 
@@ -467,8 +434,6 @@ def deps(ops):
                         pred[i][j] = True
         for r, wr in use:
             seen.setdefault(r[0], []).append((i, r[1], r[2], wr))
-        if "after" in o:
-            pred[i].setdefault(o["after"], None)
     return pred
 
 
@@ -494,7 +459,7 @@ def rank_program(g, core, T, topo):
             assert pos[j] < pos[i]
             w = pred[i][j]
             pj = ops[j]
-            if w is None or (pj["on"] == e and pj["kind"] == "c" and (not w or e == "p")):
+            if pj["on"] == e and pj["kind"] == "c" and (not w or e == "p"):
                 continue
             key = pj["on"] if pj["kind"] == "c" else pj["sem"]
             if kn.get(key, -1) >= pos[j]:

@@ -4,51 +4,56 @@ F32, BF, F16, I32, U16 = "float32", "bfloat16", "float16", "int32", "uint16"
 _SB = [("SIN", 89, I32), ("LIN", 89, I32), ("MT", 4096, I32), ("NX", 4096, I32),
        ("PCI", 3, I32), ("PCF", 3, F32), ("TK", 1, F32), ("EF", 2, F32),
        ("G16", 128, BF), ("C16", 128, BF), ("PRI", 128, BF), ("IDN", 128, BF),
-       ("BO", 128, BF), ("BON", 128, BF), ("M16", 128, BF), ("TRI", 128, BF), ("IM", 256, BF),
-       ("DB", 144, BF), ("KC", 256, F32), ("TBC", 16, BF), ("J16", 16, F32),
+       ("BO", 128, BF), ("BON", 128, BF), ("M16", 128, BF), ("TRI", 128, BF), ("IM", 128, BF),
+       ("DB", 144, BF), ("KC", 136, F32), ("TBC", 16, BF), ("J16", 16, F32),
        ("NN", 16, F32), ("CB", 16, F32), ("SLN", 32, F32), ("SLU", 32, F16),
        ("LU", 48, U16), ("KI", 32, I32), ("KU", 32, U16), ("WF", 25, F32), ("SP", 16, F32), ("MSK", 512, BF),
        ("RL", 96, BF), ("BL", 96, BF), ("OFF", 8, U16), ("CLI", 6, I32), ("CLU", 6, U16), ("XE", 1, F32),
-       ("ZE", 4224, BF), ("ZA", 4352, BF), ("ZB", 4096, BF), ("ZQ", 2048, BF), ("ZOI", 8, I32), ("ZOU", 8, U16),
-       ("KG", 1040, F32), ("GQ", 256, F32), ("G1U", 768, U16), ("HM", 512, F16), ("QU", 32, U16),
-       ("G2", 12288, F16), ("X3", 2048, U16), ("G3", 28672, BF),
-       ("REC", 528, BF), ("SA", 544, BF), ("KR", 1056, BF), ("KS", 1056, BF), ("TQ", 256, BF), ("TS", 256, BF), ("RQ1", 256, BF),
-       ("OWN", 256, BF), ("ZZ", 1152, BF), ("TK2", 1, F32),
-       ("SQ0", 528, BF), ("SQ1", 528, BF), ("SQQ", 256, BF), ("DBT", 768, F32), ("SCN", 8192, F32),
-       ("HL", 2, F32), ("UP", 32, F32), ("TT", 32, F32), ("NEW", 32, BF), ("NS", 32, F16), ("INC", 36, F16),
+       ("ZE", 4224, BF), ("ZA", 4352, BF), ("ZB", 4096, BF), ("ZQ", 2048, BF),
+       ("ZOI", 8, I32), ("ZOU", 8, U16), ("KG", 512, F32), ("GQ", 272, F32), ("NAT", 784, BF), ("NR", 256, BF), ("NL", 16, U16),
+       ("G1U", 768, U16), ("HM", 512, F16), ("QU", 32, U16), ("G2", 12288, F16), ("X3", 2048, U16), ("G3", 28672, BF),
+       ("REC", 528, BF), ("SA", 544, BF), ("KR", 528, BF), ("KS", 1552, BF), ("TQ", 272, BF), ("TS", 272, BF), ("RQ1", 256, BF),
+       ("OWN", 256, BF), ("TB", 512, BF), ("TK2", 1, F32),
+       ("SQ0", 528, BF), ("SQ1", 528, BF), ("SQQ", 256, BF), ("DBT", 1024, F32), ("SCN", 8192, F32),
+       ("UP", 32, F32), ("TT", 32, F32), ("NEW", 32, BF), ("NS", 32, F16), ("INC", 36, F16),
        ("SCU", 16, U16), ("CMU", 32, U16), ("MSG", 48, F16),
-       ("C1", 1, F32), ("NE", 512, BF), ("NC", 2, F32), ("RH", 32, BF), ("MN", 2, F32), ("WS", 256, BF),
+       ("C1", 1, F32), ("NE", 512, BF), ("NC", 2, F32), ("RH", 32, BF), ("MN", 2, F32), ("WS", 128, BF),
        ("PJ", 20, I32), ("PU", 10, U16),
-       ("RKR", 528, BF), ("RKS", 1552, BF), ("RQ", 256, BF), ("RS", 256, BF), ("RMS", 48, F16), ("RWS", 128, BF),
-       ("RSU", 16, U16), ("FIN", 1552, F32), ("YM", 512, F32), ("FL", 768, F32), ("FE", 16, F32)]
+       ("RKR", 528, BF), ("RQ", 256, BF), ("RMS", 48, F16), ("RFL", 52, F32), ("WD", 144, BF),
+       ("RSU", 32, U16), ("FIN", 1552, F32), ("YM", 512, F32), ("FL", 52, F32)]
 SCRATCH = {n: ("sbuf", [128, w], d) for n, w, d in _SB}
 for _b in range(8):
     SCRATCH["PS%d" % _b] = ("psum", [128, 512], F32)
 SEMAPHORES = (["cv", "ca", "cp", "cg", "lsem"] + ["d%d" % i for i in range(24)] + ["r%d" % i for i in range(8)])
 
 U = 1.0 / 2048
-CHUNKS = (1024, 1024, 1024, 512, 512)
-PA = ((0, 32, 32), (32, 32, 32), (64, 64, 64), (128, 128, 128), (256, 128, 64), (384, 128, 64))
-PB = ((0, 128, 64), (128, 128, 128), (256, 128, 128), (384, 128, 64))
-PC = ((256, 128, 64), (384, 128, 128))
-PD = ((512, 128, 64), (640, 64, 64), (704, 64, 32))
-PE = ((0, 128, 64), (128, 128, 128), (512, 128, 128), (640, 128, 64))
-S2 = 64
-MB = ((0, 1, 3, 4), (0, 1, 3, 4))
+CHUNKS = (512, 1024, 1024, 1024, 512)
+PASS = (0, 512, 1024, 1536, 2048, 2560, 3072, 3584, 3840, 4096)
+PA = ((-1, 0, 64, 0), (0, 0, 64, 3), (0, 0, (64,), 4), (-1, 64, 64, 0), (0, 64, 64, 0), (0, 64, (64,), 1),
+      (-1, 128, 128, 0), (0, 128, 128, 3), (0, 128, (128,), 4))
+PA2 = ((-1, 256, 128, 0), (0, 256, 128, 0), (0, 256, (128,), 1), (-1, 384, 128, 0), (0, 384, 128, 3), (0, 384, (64, 64), 4))
+PB = ((1, 0, 256, 5), (1, 0, (128, 128), 16), (1, 256, 256, 5), (1, 256, (64, 64, 64, 64), 16))
+PC = ((2, 256, 256, 5), (2, 256, (128, 64, 64), 6))
+PD = ((-1, 512, 128, 0), (0, 512, 128, 3), (0, 512, (64, 64), 4), (-1, 640, 64, 0), (0, 640, 64, 0), (0, 640, (64,), 1),
+      (-1, 704, 64, 0), (0, 704, 64, 3), (0, 704, (32, 32), 4))
+PE = ((2, 0, 256, 5), (2, 0, (64, 128), 6), (2, 192, (64,), 6), (2, 512, 128, 5), (2, 640, 128, 5), (2, 512, (64, 64), 6),
+      (2, 640, (64,), 5), (2, 704, (64,), 6))
+PW = 64
+MB = (0, 1, 3, 4)
 ORDER = """
-1 7 2 3 4 15 0 14 34a 10 9 42 23 22 21 24 62v 54 31 32 20 12 8 13 11 61 37 26 33a 35v 36v 57v 55v 29 60v 58v 28 27 66v
-25 30 56v 19v 38v 59 68 69 67 65 64 70 78 79 82v 91 88 89 71 83 72 84 49 17 16 18 41 48 40 5 6 74 76 87 85 97 90 73 80
-96 109a 115a 81 92 103 98 104 99 121 100 110 105 101 111 93 122a 133a 75 43 116 123 199 117 77 124 112 125 118 134 200
-201 106v 113 135 114v 142 107 108v 205 126 119 136 120 141 206 127v 137v 143 144 86v 146v 202v 138 128 145 210 129 139
-140 130 50 46 51 47 45 39 147 149 211 102v 158 160 154 131 215 159 148v 166 156 207 161 155 162 203 150 168 132 204 151
-167 157 163 94 52 53 44 216 164 174 170 208 169 175 165 218v 172 176 171 177 182 246 173 247 152 178 184 180 212 153
-217 183 209v 181 185 179 95 186 249 252 253 188 63v 189 190 213 191 214v 187 192 193 195v 198 194 219 281 220v 221 197
-225 282 222 226 223 227 228 224 229 248v 254 273a 267a 287 250 251 231 230 232 260 288 233 235 255 236v 234 239 259a
-256v 237 238v 257 261 268 258 262 269 292 274 264v 293 283 240 241 263 270 265 271 266 242 289 275 284v 276v 305 272v
-285 314 310 312 277v 278 286v 315 313 311 279 294 322 320 316 306 317 297 318 324 290 323 298 321 307 291 299 325 319
-328 332 330 329 331 326 295 338 333 327 340 243 341 339 308 336 334 335 337 300 296 301 245 359 244 309 342 358 366 196
-280 304 302 344 343 346 345 347 351 348 349 352 353 354 355 303 350 356 357 363 364 365 360 361 362 369 371 367 368 374
-370v 375v 376 372 373
+1 2 3 15 0 7 9 14 56 12 51 41 10 21 22 23 63v 19 20 16v 34 25 65 18v 57 61v 30 8 24 31 60v 29 33v 27v 45 11 13 35 32 17
+59 26 70 71 42 58v 36v 37 69v 64 68v 74 72 66 67 62 4 76 89a 97 48 50 88a 28v 38 49 52 47 95 96 55 39 46 53 44 40 101a
+92 93 5 82 80 6 84 75 73 78v 98 99 79 100 77 90 103 102 86v 106a 91a 107 125a 83 81 113 193 108 109 110a 94 111a 114
+119 194 115a 126 195 127 138a 120 196 121a 128a 197a 87 85 146 116v 129v 122 139 140 141a 198 207 117 123 124v 118 142v
+147 208 148 209 210 149 199 130 131 200 150 201 211 132v 143 144 133 145 215 202 203 104 247 248 249 134 135 136 213
+151v 204v 212v 155 152 153 137 205 162 250 154 206 251a 164 160 214v 163 156 166 216 284 217 165 161 167 172 218 168
+170 219 174 285 173 171 169 175 157 252 220 158 221 286 159 222v 287 253 288a 254 176 105 178 177 180 179 181 227 43 54
+255 182 183 185v 187 188 189 228 184 229 112v 256 190 191 230 231 192v 232 223 233 257 258 259v 234 237 224 238v 225
+235 289 291 239 290 292 293 226 236 261 270a 271 272 241v 240 246 374 375 384 381 276a 242 262 263 264a 265 298 273v
+266v 243 277 278a 244 280 294v 279v 274 267 268 269v 275v 295 299 315 300 281 282v 283 324 320 316 321 304 245 301 322
+328 305 325 323 329 326 327 296 332 333 330 331 302 303a 317 297 334 340 336 306 338 335 341 337 339 342 344 348 346
+343 345 347 307 350 351 349 309 310 318 319 312 308 311 260 313 186 314 352 354 353 356 355 357 362 358 359 363a 364a
+365 360 368 366 367 371 369 361 372 376 377 370 378 373 379 382 380 383 385
 """
 
 
@@ -98,6 +103,8 @@ def build(T, topo, core):
         def fn(q, e):
             if e == "v":
                 return q.tensor_copy(ap(o), ap(i))
+            if e == "g":
+                return q.affine_select(ap(o), ap(i), [[0, o[2] - o[1]]], Alu.is_ge, 0.0, 0, 0)
             return q.activation(ap(o), ap(i), Act.Copy)
         add(eng, fn, o, [i])
 
@@ -114,8 +121,16 @@ def build(T, topo, core):
     def ms(o, v):
         add("v", lambda q, e: q.memset(ap(o), v), o, [])
 
-    def red(o, i, op, neg=False):
-        add("v", lambda q, e: q.tensor_reduce(ap(o), ap(i), Ax.X, op, negate=neg), o, [i])
+    def red(o, i, op):
+        add("v", lambda q, e: q.tensor_reduce(ap(o), ap(i), Ax.X, op), o, [i])
+
+    def count(o, i):
+        def fn(q, e):
+            if e == "v":
+                return q.tensor_reduce(ap(o), ap(i), Ax.X, Alu.add, negate=True)
+            return q.activation(ap(i), ap(i), Act.Identity, scale=-1.0, accum_out=ap(o))
+        add("va", fn, o, [i])
+        ops[-1]["w"].append(i)
 
     def scan(o, d0, d1, init, op0, op1):
         add("v", lambda q, e: q.tensor_tensor_scan(ap(o), ap(d0), ap(d1), sc(init), op0, op1), o, [d0, d1, init])
@@ -141,8 +156,8 @@ def build(T, topo, core):
             return q.iota(ap(o), pat, base, cm, allow_small_or_imprecise_dtypes=True)
         add("g", fn, o, [])
 
-    def pick(o, i, pat, op, cm):
-        add("g", lambda q, e: q.affine_select(ap(o), ap(i), pat, op, 0.0, 0, cm), o, [i])
+    def pick(o, i, pat, op, cm, fill=0.0):
+        add("g", lambda q, e: q.affine_select(ap(o), ap(i), pat, op, fill, 0, cm), o, [i])
 
     def fill1(o, v):
         n = o[2] - o[1]
@@ -151,13 +166,14 @@ def build(T, topo, core):
             if e == "v":
                 return q.memset(ap(o), float(v))
             if e == "a":
-                return q.activation(ap(o), T.ZZ[:, 0:n], Act.Identity, bias=float(v))
+                return q.activation(ap(o), T.ZE[:, 0:n], Act.Copy)
             return q.iota(ap(o), [[0, n]], v, 0, allow_small_or_imprecise_dtypes=True)
-        add("gav", fn, o, [("ZZ", 0, 1152)])
+        eng = {"ZE": ("v", "av", "av", "av"), "ZA": ("g", "av", "av", "g")}.get(o[0], "gggg")[o[1] // 1088]
+        add(eng, fn, o, [("ZE", 0, 1088)] if eng == "av" else [])
 
     def fill(name, lo, hi, v=0):
-        for a in range(lo, hi, 1152):
-            fill1((name, a, min(hi, a + 1152)), v)
+        for a in range(lo, hi, 1088):
+            fill1((name, a, min(hi, a + 1088)), v)
 
     def dma(eng, prs, w, rd):
         s = "d%d" % cnt["d"]
@@ -201,7 +217,6 @@ def build(T, topo, core):
     iota(("PRI", 0, 128), [[0, 128]], 1, 0)
     pick(IDN, ("PRI", 0, 128), [[-1, 128]], Alu.is_equal, 1)
     iota(("J16", 0, 16), [[16, 16]], 0, 0)
-    ms(("ZZ", 0, 1152), 0.0)
     fill("ZE", 0, 4224)
     ms(("DB", 0, 144), 0.0)
     ms(("INC", 0, 1), 16.0 * U)
@@ -211,7 +226,7 @@ def build(T, topo, core):
     cp(("CLU", 0, 6), ("CLI", 0, 6))
     lin(("XE", 0, 1), PI, 128.0, PG)
     for s, o in enumerate((2176.0, 2304.0, 2048.0)):
-        ts(("OFF", 2 * s + 1, 2 * s + 2), ("XE", 0, 1), o, None, Alu.add)
+        lin(("OFF", 2 * s + 1, 2 * s + 2), ("XE", 0, 1), 1.0, o)
     cp(("OFF", 6, 7), PP)
     ts(BO, ("G16", 0, 128), PG, None, Alu.is_equal)
     ts(("M16", 0, 128), ("C16", 0, 128), PI, None, Alu.is_equal)
@@ -223,13 +238,17 @@ def build(T, topo, core):
     fill1(("ZQ", 1024, 2048), 0)
     iota(("ZOI", 0, 8), [[128, 8]], 0, 1)
     cp(("ZOU", 0, 8), ("ZOI", 0, 8))
-    fill("KG", 256, 1040)
+    fill("NAT", 0, 784, 256)
+    iota(("NR", 0, 256), [[1, 256]], 0, 0)
+    fill("GQ", 256, 272)
     fill("ZB", 0, 4096)
     fill("SA", 272, 288, -1)
-    fill("KR", 272, 1056, -1)
-    fill("KS", 272, 1056, -1)
+    fill("TQ", 256, 272, -1)
+    fill("TS", 256, 272, -1)
+    fill("KS", 528, 1552, -1)
     fill("FIN", 528, 1552, -1)
-    fill("RKS", 528, 1552, -1)
+    fill("WD", 0, 144)
+    fill("FL", 48, 52)
     lin(("NN", 0, 16), ("J16", 0, 16), 1.0, PI)
     lin(("CB", 0, 16), ("NN", 0, 16), 1.0 / 512, 256.0)
     for t, top in ((0, 272.0), (1, 512.0)):
@@ -239,49 +258,44 @@ def build(T, topo, core):
     lin(("EF", 0, 2), ("M16", 0, 2), -1.0, 1.0)
     lin(("TK2", 0, 1), PI, 1.0 / 8192, 0.0)
     lin(("TBC", 0, 16), E16, ("TK2", 0, 1), 0.0)
-    for t in range(2):
-        lin(("KC", 128 * t, 128 * t + 128), dd(t), ("TK", 0, 1), -1000.0)
-        lin(("IM", 128 * t, 128 * t + 128), IDN, ("EF", t, t + 1), 0.0)
+    lin(("KC", 0, 128), dd(0), ("TK", 0, 1), -1000.0)
+    lin(("IM", 0, 128), IDN, ("EF", 0, 1), 0.0)
+    lin(("KC", 128, 136), ("BO", 0, 128, 16), ("TK", 0, 1), -1000.0)
 
-    for lo, hi in zip(cuts, cuts[1:]):
+    for lo, hi in zip(PASS, PASS[1:]):
         lin(("NX", lo, hi), ("MT", lo, hi), 0.0625, -0.46875)
         ts(("MT", lo, hi), ("MT", lo, hi), 15, None, Alu.bitwise_and)
 
-    cp(("LU", 0, 48), ("LIN", 0, 48))
-    cp(("WF", 0, 25), ("LIN", 64, 89))
+    cp(("LU", 0, 48), ("LIN", 0, 48), "va")
+    cp(("WF", 0, 25), ("LIN", 64, 89), "va")
     ts(("KI", 0, 16), ("LIN", 48, 64), 6, None, Alu.arith_shift_right)
-    cp(("KU", 0, 16), ("KI", 0, 16))
+    cp(("KU", 0, 16), ("KI", 0, 16), "va")
     cp(("MSK", 0, 256), ind(E16, ("LU", 16, 32)), "av")
     cp(("MSK", 256, 512), ind(E16, ("LU", 32, 48)), "av")
     lin(("SP", 0, 16), ("WF", 0, 16), 0.125, 0.0)
-    cp(("REC", 0, 16), ("WF", 3, 19), "av")
-    cp(("SA", 0, 16), ("WF", 6, 22), "av")
-    cp(("KS", 0, 16), ("WF", 9, 25), "av")
+    cp(("REC", 0, 16), ("WF", 3, 19), "gav")
+    cp(("SA", 0, 16), ("WF", 6, 22), "gav")
+    cp(("KS", 0, 16), ("WF", 9, 25), "gav")
     ZS = (("ZE", 2176, 4224), ("ZA", 2304, 4352), ("ZB", 2048, 4096))
     tt(("RL", 0, 96), ind(("WF", 16, 25), ("CLU", 0, 6)), ("M16", 0, 96), Alu.mult)
     acc(ps(2, 256, 352), [(BO, ("RL", 0, 96))])
     ts(("BL", 0, 96), ps(2, 256, 352), PI, None, Alu.is_equal)
-    ts(("OFF", 0, 6, 2), ("WF", 16, 25, 3), 128.0, PP, Alu.mult, Alu.add)
+    lin(("OFF", 0, 6, 2), ("WF", 16, 25, 3), 128.0, PP, "va")
     for s in range(3):
         cp(ind((ZS[s][0], 0, ZS[s][2]), ("OFF", 2 * s, 2 * s + 2)), ("BL", 32 * s, 32 * s + 32))
     cp(ind(("ZA", 2176, 2304), ("OFF", 6, 7)), ("BL", 48, 64))
     WNX, WOT = ("NX", 0, 4096), ("MT", 0, 4096)
 
     def step1(lst, k0, keep):
-        cp(("G1U", k0, k0 + 256), ind(WNX, lst))
+        cp(("G1U", k0, k0 + 256), ind(WNX, lst), "va")
         if keep is not None:
-            lin(keep, ind(WNX, lst), 1.0, -2048.0)
+            lin(keep, ("G1U", k0, k0 + 256), 1.0, -2048.0)
 
     def queries(t):
         tt(("HM", 256 * t, 256 * t + 256), ind(("KG", 0, 256 * (t + 1)), ("KU", 16 * t, 16 * t + 16)), ("MSK", 256 * t, 256 * t + 256), Alu.mult)
         acc(ps(2, 0, 16), [(dd(i), ("HM", 256 * t + i, 256 * t + 256, 16)) for i in range(16)])
-        ts(("QU", 16 * t, 16 * t + 16), ps(2, 0, 16), 2048.0, None, Alu.add)
+        lin(("QU", 16 * t, 16 * t + 16), ps(2, 0, 16), 1.0, 2048.0, "va")
         step1(("QU", 16 * t, 16 * t + 16), 256 * (t + 1), ("GQ", 0, 256) if t == 0 else None)
-
-    def step2(k0, w):
-        for u in range(k0, k0 + w, S2):
-            v = min(u + S2, k0 + w)
-            lin(("G2", 16 * u, 16 * v), ind(WNX, ("G1U", u, v)), 1.0, -2048.0, "va")
 
     def dest(s, k):
         if s == 0:
@@ -290,56 +304,85 @@ def build(T, topo, core):
             return ("SA", 16 + k if k < 256 else 32 + k)
         return (("KS", 16 + k), ("TS", k - 256), ("OWN", k - 512))[k // 256]
 
-    def walk(s, k0, w, sub):
-        b2, b3 = ((3, 4), (0, 1))[cnt["w"] % 2] if s == 0 else (5, 6)
-        cnt["w"] += s == 0
+    def pick2(s, k0, w, b):
+        x0 = (0, 768, 1280)[s] + k0
+        for u in range(0, w, PW):
+            v = min(u + PW, w)
+            acc(ps(b, u, v), [((ZS[s][0], 128 * a, 128 * a + 128), ("G2", 16 * (k0 + u) + a, 16 * (k0 + v), 16)) for a in range(16)])
+        lin(("X3", x0, x0 + w), ps(b, 0, w), 1.0, 2048.0, "va")
+
+    def pick3(s, k0, subs, b):
         x0 = (0, 768, 1280)[s] + k0
         y0 = (k0 % 512, 512 + k0, 1024 + k0)[s]
-        acc(ps(b2, 0, w), [((ZS[s][0], 128 * a, 128 * a + 128), ("G2", 16 * k0 + a, 16 * (k0 + w), 16)) for a in range(16)])
-        ts(("X3", x0, x0 + w), ps(b2, 0, w), 2048.0, None, Alu.add)
-        for u in range(0, w, sub):
-            cp(("G3", 16 * (y0 + u), 16 * (y0 + u + sub)), ind(WOT, ("X3", x0 + u, x0 + u + sub)), "av")
+        w = 0
+        for sub in subs:
+            cp(("G3", 16 * (y0 + w), 16 * (y0 + w + sub)), ind(WOT, ("X3", x0 + w, x0 + w + sub)), "av")
+            w += sub
         z, o = ZS[s][:2]
-        acc(ps(b3, 0, w), [((z, o + 127 * e, o + 127 * e + 128), ("G3", 16 * y0 + e, 16 * (y0 + w), 16)) for e in range(16)])
+        if b > 9:
+            b -= 10
+            t0 = 256 * (cnt["w"] % 2)
+            cnt["w"] += 1
+            for u in range(0, w, 128):
+                for h in (0, 8):
+                    mm([(ps(b, 256 + u + e, 384 + u, 16), ("G3", 16 * (y0 + u) + e, 16 * (y0 + u + 128), 16),
+                         (z, o + 128 * e, o + 128 * e + 128, 16), True, True) for e in range(h, h + 8)])
+            cp(("TB", t0, t0 + w), ps(b, 256, 256 + w), "av")
+            mm([(ps(b, u, u + 128), ("TB", t0 + u, t0 + u + 128), IDN, True, True) for u in range(0, w, 128)])
+        else:
+            for u in range(0, w, PW):
+                v = min(u + PW, w)
+                acc(ps(b, u, v), [((z, o + 127 * e, o + 127 * e + 128), ("G3", 16 * (y0 + u) + e, 16 * (y0 + v), 16)) for e in range(16)])
         d, c0 = dest(s, k0)
-        cp((d, c0, c0 + w), ps(b3, 0, w), "av")
+        cp((d, c0, c0 + w), ps(b, 0, w), "av")
+
+    def walks(plan):
+        for s, k0, x, b in plan:
+            if s < 0:
+                lin(("G2", 16 * k0, 16 * (k0 + x)), ind(WNX, ("G1U", k0, k0 + x)), 1.0, -2048.0, "va")
+            elif isinstance(x, int):
+                pick2(s, k0, x, b)
+            else:
+                pick3(s, k0, x, b)
 
     def known_side(t, src, sq):
         n = 256 * (t + 1)
         square((sq, 15, 16 + n), (src, 15, 16 + n))
         acc(ps(7, 0, n), [(BO, (sq, 16, 16 + n)), (("BON", 0, 128), (sq, 15, 15 + n))])
-        lin(("DBT", 256 * t, 256 * t + n), ps(7, 0, n), 1.0, U)
+        lin(("DBT", 512 * t, 512 * t + n), ps(7, 0, n), 1.0, U)
+        if t == 0:
+            pick(("DBT", 256, 512), ("DBT", 0, 256), [[1, 256]], Alu.is_gt, 0, -1.0e9)
         acc(ps(7, 0, 2), [(BO, (sq, 14 + n, 16 + n))])
-        lin(("HL", t, t + 1), ps(7, 1, 2), 1.0, (n - 1) * U)
-
-    def spread(rq, lo, hi):
-        cp(ind(("ZQ", 8 * lo, 8 * hi), ("ZOU", 0, 8)), (rq[0], rq[1] + lo, rq[1] + hi))
 
     def match(t, rq, sq, known):
         n = 256 * (t + 1)
         c = (16 * t, 16 * t + 16)
-        spread(rq, 0, 128)
-        spread(rq, 128, 256)
+        for lo in (0, 128):
+            cp(ind(("ZQ", 8 * lo, 8 * lo + 1024), ("ZOU", 0, 8)), (rq[0], rq[1] + lo, rq[1] + lo + 128))
         square(sq, rq)
         acc(ps(2, 0, 16), [(dd(i), (sq[0], sq[1] + i, sq[2], 16)) for i in range(16)])
-        lin(("UP",) + c, ps(2, 0, 16), 1.0, ("HL", t, t + 1))
-        for j in range(16):
-            b = MB[t][j % len(MB[t])]
-            acc(ps(b, 0, n), [(("ZQ", 128 * j, 128 * j + 128), (known, 16, 16 + n))])
-            scan(("SCN", 512 * j, 512 * j + n), ("DBT", 256 * t, 256 * t + n), ps(b, 0, n), -1.0e9, Alu.add, Alu.max)
-        tt(("TT",) + c, ("UP",) + c, ("SCN", n - 1, 8192, 512), Alu.subtract)
+        ts(("UP",) + c, ps(2, 0, 16), ps(7, 1, 2), (n - 1) * U, Alu.add, Alu.add)
+        m = 512 // n
+        for j in range(0, 16, m):
+            b = MB[j // m % len(MB)]
+            mm([(ps(b, n * i, n * i + n), ("ZQ", 128 * (j + i), 128 * (j + i + 1)), (known, 16, 16 + n), True, True) for i in range(m)])
+            scan(("SCN", n * j, n * j + 512), ("DBT", 512 * t, 512 * t + 512), ps(b, 0, 512), -1.0e9, Alu.add, Alu.max)
+        tt(("TT",) + c, ("UP",) + c, ("SCN", n - 1, 16 * n, n), Alu.subtract)
         ts(("CMU",) + c, ("TT",) + c, 2048.0, float(n), Alu.mult, Alu.min)
-        ts(("NEW",) + c, ("TT",) + c, 0.4, U, Alu.is_ge, Alu.mult)
+
+    def places(t):
+        c = (16 * t, 16 * t + 16)
         i0 = 18 * t
+        ts(("NEW",) + c, ("TT",) + c, 0.4, U, Alu.is_ge, Alu.mult)
         scan(("INC", i0 + 1, i0 + 17), ("NEW",) + c, ("NEW",) + c, 16.0 * U if t == 0 else ("C1", 0, 1), Alu.add, Alu.max)
         tt(("NS",) + c, ("NEW",) + c, ("SLN",) + c, Alu.mult)
         p = ps(2, 0, 16)
         mm([(ps(2, 0, 17), BO, ("INC", i0, i0 + 17), True, False), (p, IDN, ("SLU",) + c, False, False),
             (p, ("TRI", 0, 128), ("NEW",) + c, False, False), (p, IDN, ("NS",) + c, False, True)])
+        lin((("SCU", "RSU")[t], 0, 16), p, 2048.0, -256.0, "va")
         if t == 0:
-            ts(("SCU", 0, 16), p, 2048.0, -256.0, Alu.mult, Alu.add)
             ts(("KI", 16, 32), ("SP", 0, 16), ps(2, 16, 17), -0.499969482421875, Alu.mult, Alu.add)
-            cp(("KU", 16, 32), ("KI", 16, 32))
+            cp(("KU", 16, 32), ("KI", 16, 32), "va")
             lin(("C1", 0, 1), ps(2, 16, 17), 1.0 / 16, 0.0)
             cp(("INC", 18, 19), ("C1", 0, 1), "av")
         else:
@@ -350,57 +393,57 @@ def build(T, topo, core):
         n = 256 * (t + 1)
         ne = ("NE", 256 * t, 256 * t + 256)
         tt(ne, ind((src, 16, 32 + n), ("CMU", 16 * t, 16 * t + 16)), own, Alu.not_equal)
-        red(("NC", t, t + 1), ne, Alu.add, True)
+        count(("NC", t, t + 1), ne)
         lin(("RH", 16 * t, 16 * t + 16), E16, ("NC", t, t + 1), 0.0, "va")
         acc(ps(7, 0, 16), [(BO, ("RH", 16 * t, 16 * t + 16)), (BO, ("TBC", 0, 16))])
         red(("MN", t, t + 1), ps(7, 0, 16), Alu.min)
-        ts(("WS", 128 * t, 128 * t + 128), ("KC", 128 * t, 128 * t + 128), ("NC", t, t + 1), ("MN", t, t + 1), Alu.add, Alu.is_equal)
+        ts((("WS", 0, 128), ("WD", 15, 143, 16))[t], ("KC", 128 * t, (128, 136)[t]), ("NC", t, t + 1), ("MN", t, t + 1), Alu.add, Alu.is_equal)
 
     step1(("LU", 0, 16), 0, ("KG", 0, 256))
     queries(0)
-    for k0, w, sub in PA:
-        step2(k0, w)
-        walk(0, k0, w, sub)
-        if k0 + w == 256:
-            known_side(0, "REC", "SQ0")
+    walks(PA)
+    known_side(0, "REC", "SQ0")
+    walks(PA2)
     match(0, ("REC", 272, 528), ("SQ0", 272, 528), "REC")
-    cp(ind(("KG", 256, 1040), ("SCU", 0, 16)), ("GQ", 0, 256))
-    for x in PB:
-        walk(1, *x)
+    places(0)
+    send(client, ("RMS", 0, 16), ("MSG", 0, 16))
+    cp(ind(("NAT", 0, 784), ("SCU", 0, 16)), ("NR", 0, 256))
+    acc(ps(2, 0, 16), [(dd(i), ("NAT", i, 256, 16)) for i in range(16)])
+    lin(("NL", 0, 16), ps(2, 0, 16), 1.0 / 16, 0.0, "va")
+    cp(("KG", 256, 512), ind(("GQ", 0, 272), ("NL", 0, 16)), "av")
+    walks(PB)
     queries(1)
     winner(0, "SA", ("SA", 288, 544))
     ts(("PJ", 0, 9), ("CB", 0, 9), ("MN", 0, 1), 8192.0, Alu.add, Alu.mult)
     ts(("PJ", 10, 19), ("PJ", 0, 9), 8191, None, Alu.bitwise_and)
-    cp(("PU", 0, 9), ("PJ", 10, 19))
+    cp(("PU", 0, 9), ("PJ", 10, 19), "va")
     cp(("ZE", 0, 2304, 16), ind(("ZA", 0, 2304), ("PU", 0, 9)), "va")
     acc(ps(7, 0, 256), [(("IM", 0, 128), ("REC", 272, 528)), (("WS", 0, 128), ("SA", 288, 544))])
     cp(("TQ", 0, 256), ps(7, 0, 256), "av")
     acc(ps(7, 0, 272), [(("IM", 0, 128), ("REC", 0, 272)), (("WS", 0, 128), ("SA", 0, 272))])
     cp(("KR", 0, 272), ps(7, 0, 272), "av")
-    cp(ind(("KR", 272, 1056), ("SCU", 0, 16)), ("TQ", 0, 256))
+    cp(("KR", 272, 528), ind(("TQ", 0, 272), ("NL", 0, 16)), "av")
     known_side(1, "KR", "SQ1")
     send(client, ("RKR", 0, 528), ("KR", 0, 528))
-    for x in PC:
-        walk(2, *x)
-    cp(ind(("KS", 272, 1056), ("SCU", 0, 16)), ("TS", 0, 256))
-    send(client, ("RKS", 272, 528), ("KS", 272, 528))
-    for k0, w, sub in PD:
-        step2(k0, w)
-        walk(0, k0, w, sub)
+    walks(PC)
+    cp(("KS", 272, 528), ind(("TS", 0, 272), ("NL", 0, 16)), "av")
+    walks(PD)
     send(client, ("RQ", 0, 256), ("RQ1", 0, 256))
-    for x in PE:
-        walk(2, *x)
-    send(client, ("RS", 0, 256), ("OWN", 0, 256))
-    send(client, ("RKS", 0, 272), ("KS", 0, 272))
+    walks(PE)
     match(1, ("RQ1", 0, 256), ("SQQ", 0, 256), "KR")
-    send(client, ("RMS", 0, 48), ("MSG", 0, 48))
+    places(1)
+    send(client, ("RMS", 16, 48), ("MSG", 16, 48))
     winner(1, "KS", ("OWN", 0, 256))
-    send(client, ("RWS", 0, 128), ("WS", 128, 256))
-    cp(("FIN", 16, 272), ("RKR", 16, 272), "av")
-    cp(("FIN", 272, 528), ("RKR", 272, 528), "av")
-    ts(("RSU", 0, 16), ("RMS", 32, 48), 2048.0, -256.0, Alu.mult, Alu.add)
-    cp(ind(("RKS", 272, 1552), ("RSU", 0, 16)), ("RS", 0, 256))
-    cp(ind(("FIN", 272, 1552), ("RSU", 0, 16)), ("RQ", 0, 256))
+    cp(ind(("KS", 272, 1552), ("RSU", 0, 16)), ("OWN", 0, 256))
+    acc(ps(3, 0, 48), [(("WD", 15 - i, 143 - i), ("KS", 16 + 48 * i, 64 + 48 * i)) for i in range(16)])
+    cp(("FL", 0, 48), ps(3, 0, 48), "av")
+    acc(ps(4, 0, 4, 1, 8), [(("WD", 15, 143, 16), ("KS", 12, 16))])
+    cp(("FL", 48, 52, 1, 8), ps(4, 0, 4, 1, 8), "va")
+    send(client, ("RFL", 0, 52), ("FL", 0, 52))
+    cp(("FIN", 12, 272), ("RKR", 12, 272), "gav")
+    cp(("FIN", 272, 528), ("RKR", 272, 528), "gav")
+    lin(("RSU", 16, 32), ("RMS", 32, 48), 2048.0, -256.0, "va")
+    cp(ind(("FIN", 272, 1552), ("RSU", 16, 32)), ("RQ", 0, 256))
     mm([(ps(7, i, 512, 16, 8), ("IDN", i, 128, 16), ("RMS", 0, 32), True, True) for i in range(16)])
     lin(("YM", 0, 512, 1, 8), ps(7, 0, 512, 1, 8), 2048.0, 0.0)
     dma("s", [(T.ym[:, :], T.YM[0:8, :])], ("ym", 0, 512), [("YM", 0, 512)])
@@ -408,13 +451,8 @@ def build(T, topo, core):
     dma("s", [(T.yr[a:b, 0:256], T.FIN[a:b, 16:272]) for a, b in rows], ("yr0", 0, 1), [("FIN", 16, 272)])
     for q, part in (("s", rows[:5]), ("a", rows[5:])):
         dma(q, [(T.yr[a:b, 256:768], T.FIN[a:b, 272:784]) for a, b in part], ("yr" + q, 0, 1), [("FIN", 272, 784)])
-    for b, lo in ((3, 0), (4, 384)):
-        acc(ps(b, 0, 384, 1, 8), [(("RWS", 1, 128, 16), ("RKS", 16 + lo, 400 + lo))])
-        cp(("FL", lo, lo + 384, 1, 8), ps(b, 0, 384, 1, 8), "av")
-    dma("s", [(T.yr[1:128:16, :], T.FL[0:8, :])], ("yr1", 0, 1), [("FL", 0, 768)])
-    acc(ps(2, 0, 16), [(("IM", 128, 256), ("RKR", 0, 16)), (("RWS", 0, 128), ("RKS", 0, 16))])
-    cp(("FE", 0, 16), ps(2, 0, 16), "av")
-    dma("s", [(T.ye[:, :], T.FE[:, 13:16])], ("ye", 0, 1), [("FE", 0, 16)])
+    dma("s", [(T.ye[a:b, :], T.FIN[a:b, 13:16]) for a, b in rows], ("ye0", 0, 1), [("FIN", 12, 16)])
+    dma("s", [(T.yr[1:128:16, :], T.RFL[:, 0:48]), (T.ye[1:128:16, :], T.RFL[0:8, 49:52])], ("yr1", 0, 1), [("RFL", 0, 52)])
     return ops
 
 

from concourse.mybir import AluOpType as Alu, AxisListType as Ax, ActivationFunctionType as Act

F32, BF, F16, I32, U16 = "float32", "bfloat16", "float16", "int32", "uint16"
_SB = [("SIN", 89, I32), ("LIN", 89, I32), ("MT", 4096, I32), ("NX", 4096, I32),
       ("PCI", 3, I32), ("PCF", 3, F32), ("TK", 1, F32), ("EF", 2, F32),
       ("G16", 128, BF), ("C16", 128, BF), ("PRI", 128, BF), ("IDN", 128, BF),
       ("BO", 128, BF), ("BON", 128, BF), ("M16", 128, BF), ("TRI", 128, BF), ("IM", 128, BF),
       ("DB", 144, BF), ("KC", 136, F32), ("TBC", 16, BF), ("J16", 16, F32),
       ("NN", 16, F32), ("CB", 16, F32), ("SLN", 32, F32), ("SLU", 32, F16),
       ("LU", 48, U16), ("KI", 32, I32), ("KU", 32, U16), ("WF", 25, F32), ("SP", 16, F32), ("MSK", 512, BF),
       ("RL", 96, BF), ("BL", 96, BF), ("OFF", 8, U16), ("CLI", 6, I32), ("CLU", 6, U16), ("XE", 1, F32),
       ("ZE", 4224, BF), ("ZA", 4352, BF), ("ZB", 4096, BF), ("ZQ", 2048, BF),
       ("ZOI", 8, I32), ("ZOU", 8, U16), ("KG", 512, F32), ("GQ", 272, F32), ("NAT", 784, BF), ("NR", 256, BF), ("NL", 16, U16),
       ("G1U", 768, U16), ("HM", 512, F16), ("QU", 32, U16), ("G2", 12288, F16), ("X3", 2048, U16), ("G3", 28672, BF),
       ("REC", 528, BF), ("SA", 544, BF), ("KR", 528, BF), ("KS", 1552, BF), ("TQ", 272, BF), ("TS", 272, BF), ("RQ1", 256, BF),
       ("OWN", 256, BF), ("TB", 512, BF), ("TK2", 1, F32),
       ("SQ0", 528, BF), ("SQ1", 528, BF), ("SQQ", 256, BF), ("DBT", 1024, F32), ("SCN", 8192, F32),
       ("UP", 32, F32), ("TT", 32, F32), ("NEW", 32, BF), ("NS", 32, F16), ("INC", 36, F16),
       ("SCU", 16, U16), ("CMU", 32, U16), ("MSG", 48, F16),
       ("C1", 1, F32), ("NE", 512, BF), ("NC", 2, F32), ("RH", 32, BF), ("MN", 2, F32), ("WS", 128, BF),
       ("PJ", 20, I32), ("PU", 10, U16),
       ("RKR", 528, BF), ("RQ", 256, BF), ("RMS", 48, F16), ("RFL", 52, F32), ("WD", 144, BF),
       ("RSU", 32, U16), ("FIN", 1552, F32), ("YM", 512, F32), ("FL", 52, F32)]
SCRATCH = {n: ("sbuf", [128, w], d) for n, w, d in _SB}
for _b in range(8):
    SCRATCH["PS%d" % _b] = ("psum", [128, 512], F32)
SEMAPHORES = (["cv", "ca", "cp", "cg", "lsem"] + ["d%d" % i for i in range(24)] + ["r%d" % i for i in range(8)])

U = 1.0 / 2048
CHUNKS = (512, 1024, 1024, 1024, 512)
PASS = (0, 512, 1024, 1536, 2048, 2560, 3072, 3584, 3840, 4096)
PA = ((-1, 0, 64, 0), (0, 0, 64, 3), (0, 0, (64,), 4), (-1, 64, 64, 0), (0, 64, 64, 0), (0, 64, (64,), 1),
      (-1, 128, 128, 0), (0, 128, 128, 3), (0, 128, (128,), 4))
PA2 = ((-1, 256, 128, 0), (0, 256, 128, 0), (0, 256, (128,), 1), (-1, 384, 128, 0), (0, 384, 128, 3), (0, 384, (64, 64), 4))
PB = ((1, 0, 256, 5), (1, 0, (128, 128), 16), (1, 256, 256, 5), (1, 256, (64, 64, 64, 64), 16))
PC = ((2, 256, 256, 5), (2, 256, (128, 64, 64), 6))
PD = ((-1, 512, 128, 0), (0, 512, 128, 3), (0, 512, (64, 64), 4), (-1, 640, 64, 0), (0, 640, 64, 0), (0, 640, (64,), 1),
      (-1, 704, 64, 0), (0, 704, 64, 3), (0, 704, (32, 32), 4))
PE = ((2, 0, 256, 5), (2, 0, (64, 128), 6), (2, 192, (64,), 6), (2, 512, 128, 5), (2, 640, 128, 5), (2, 512, (64, 64), 6),
      (2, 640, (64,), 5), (2, 704, (64,), 6))
PW = 64
MB = (0, 1, 3, 4)
ORDER = """
1 2 3 15 0 7 9 14 56 12 51 41 10 21 22 23 63v 19 20 16v 34 25 65 18v 57 61v 30 8 24 31 60v 29 33v 27v 45 11 13 35 32 17
59 26 70 71 42 58v 36v 37 69v 64 68v 74 72 66 67 62 4 76 89a 97 48 50 88a 28v 38 49 52 47 95 96 55 39 46 53 44 40 101a
92 93 5 82 80 6 84 75 73 78v 98 99 79 100 77 90 103 102 86v 106a 91a 107 125a 83 81 113 193 108 109 110a 94 111a 114
119 194 115a 126 195 127 138a 120 196 121a 128a 197a 87 85 146 116v 129v 122 139 140 141a 198 207 117 123 124v 118 142v
147 208 148 209 210 149 199 130 131 200 150 201 211 132v 143 144 133 145 215 202 203 104 247 248 249 134 135 136 213
151v 204v 212v 155 152 153 137 205 162 250 154 206 251a 164 160 214v 163 156 166 216 284 217 165 161 167 172 218 168
170 219 174 285 173 171 169 175 157 252 220 158 221 286 159 222v 287 253 288a 254 176 105 178 177 180 179 181 227 43 54
255 182 183 185v 187 188 189 228 184 229 112v 256 190 191 230 231 192v 232 223 233 257 258 259v 234 237 224 238v 225
235 289 291 239 290 292 293 226 236 261 270a 271 272 241v 240 246 374 375 384 381 276a 242 262 263 264a 265 298 273v
266v 243 277 278a 244 280 294v 279v 274 267 268 269v 275v 295 299 315 300 281 282v 283 324 320 316 321 304 245 301 322
328 305 325 323 329 326 327 296 332 333 330 331 302 303a 317 297 334 340 336 306 338 335 341 337 339 342 344 348 346
343 345 347 307 350 351 349 309 310 318 319 312 308 311 260 313 186 314 352 354 353 356 355 357 362 358 359 363a 364a
365 360 368 366 367 371 369 361 372 376 377 370 378 373 379 382 380 383 385
"""


def build(T, topo, core):
    n_ranks = len(T.cores)
    rank = T.rank_of(core)
    owner = T.cores[(rank + 3) % n_ranks]
    client = T.cores[(rank - 3) % n_ranks]
    ops = []
    cnt = {"d": 0, "r": 0, "w": 0}

    def ap(r):
        if r[0] == "ind":
            return ap(r[1]).indirect(ap(r[2]))
        p = r[4] if len(r) > 4 else 128
        if len(r) > 3 and r[3] != 1:
            return T[r[0]][0:p, r[1]:r[2]:r[3]]
        return T[r[0]][0:p, r[1]:r[2]]

    def regs(rs):
        out = []
        for r in rs:
            if isinstance(r, tuple):
                out += [r[1], r[2]] if r[0] == "ind" else [r]
        return out

    def sc(x):
        return ap(x) if isinstance(x, tuple) else x

    def add(eng, fn, w, rd, kind="c", sem=None, n=1):
        if w[0] == "ind":
            rd = list(rd) + [w[2]]
            w = w[1]
        ops.append({"eng": eng, "fn": fn, "w": [w], "r": regs(rd), "kind": kind, "sem": sem, "n": n})

    def ts(o, i, s1, s2, op0, op1=None):
        def fn(q, e):
            if op1 is None:
                return q.tensor_scalar(ap(o), ap(i), sc(s1), None, op0)
            return q.tensor_scalar(ap(o), ap(i), sc(s1), sc(s2), op0, op1)
        add("v", fn, o, [i, s1, s2])

    def tt(o, a, b, op):
        add("v", lambda q, e: q.tensor_tensor(ap(o), ap(a), ap(b), op), o, [a, b])

    def cp(o, i, eng="v"):
        def fn(q, e):
            if e == "v":
                return q.tensor_copy(ap(o), ap(i))
            if e == "g":
                return q.affine_select(ap(o), ap(i), [[0, o[2] - o[1]]], Alu.is_ge, 0.0, 0, 0)
            return q.activation(ap(o), ap(i), Act.Copy)
        add(eng, fn, o, [i])

    def lin(o, i, scale, bias, eng="av"):
        def fn(q, e):
            if e == "v":
                return q.tensor_scalar(ap(o), ap(i), sc(scale), sc(bias), Alu.mult, Alu.add)
            return q.activation(ap(o), ap(i), Act.Identity, bias=sc(bias), scale=sc(scale))
        add(eng, fn, o, [i, scale, bias])

    def square(o, i):
        add("a", lambda q, e: q.activation(ap(o), ap(i), Act.Square, scale=0.70710678), o, [i])

    def ms(o, v):
        add("v", lambda q, e: q.memset(ap(o), v), o, [])

    def red(o, i, op):
        add("v", lambda q, e: q.tensor_reduce(ap(o), ap(i), Ax.X, op), o, [i])

    def count(o, i):
        def fn(q, e):
            if e == "v":
                return q.tensor_reduce(ap(o), ap(i), Ax.X, Alu.add, negate=True)
            return q.activation(ap(i), ap(i), Act.Identity, scale=-1.0, accum_out=ap(o))
        add("va", fn, o, [i])
        ops[-1]["w"].append(i)

    def scan(o, d0, d1, init, op0, op1):
        add("v", lambda q, e: q.tensor_tensor_scan(ap(o), ap(d0), ap(d1), sc(init), op0, op1), o, [d0, d1, init])

    def mm(items):
        def fn(q, e):
            x = None
            for o, l, r, a, b in items:
                x = q.matmul(ap(o), ap(l), ap(r), a, b)
            return x
        rd = []
        for it in items:
            rd += [it[1], it[2]]
        add("p", fn, items[0][0], rd)

    def acc(o, prs):
        mm([(o, l, r, i == 0, i == len(prs) - 1) for i, (l, r) in enumerate(prs)])

    def iota(o, pat, base, cm):
        def fn(q, e):
            if SCRATCH[o[0]][2] == I32:
                return q.iota(ap(o), pat, base, cm)
            return q.iota(ap(o), pat, base, cm, allow_small_or_imprecise_dtypes=True)
        add("g", fn, o, [])

    def pick(o, i, pat, op, cm, fill=0.0):
        add("g", lambda q, e: q.affine_select(ap(o), ap(i), pat, op, fill, 0, cm), o, [i])

    def fill1(o, v):
        n = o[2] - o[1]

        def fn(q, e):
            if e == "v":
                return q.memset(ap(o), float(v))
            if e == "a":
                return q.activation(ap(o), T.ZE[:, 0:n], Act.Copy)
            return q.iota(ap(o), [[0, n]], v, 0, allow_small_or_imprecise_dtypes=True)
        eng = {"ZE": ("v", "av", "av", "av"), "ZA": ("g", "av", "av", "g")}.get(o[0], "gggg")[o[1] // 1088]
        add(eng, fn, o, [("ZE", 0, 1088)] if eng == "av" else [])

    def fill(name, lo, hi, v=0):
        for a in range(lo, hi, 1088):
            fill1((name, a, min(hi, a + 1088)), v)

    def dma(eng, prs, w, rd):
        s = "d%d" % cnt["d"]
        cnt["d"] += 1

        def fn(q, e):
            for o, i in prs:
                q.dma_start(o, i).then_inc(T.sem[s], 16)
        add(eng, fn, w, rd, "d", s, 16 * len(prs))

    def send(dst, o, i):
        s = "r%d" % cnt["r"]
        cnt["r"] += 1
        rid, pid, _ = topo.addr(dst)
        add("g", lambda q, e: q.remote_dma(ap(o), ap(i), T.sem[s], T.sem.lsem, pid, rid, topo.mask(core, dst)),
            o, [i], "r", s, len(topo.engines(core, dst)))

    def ind(w, o):
        return ("ind", w, o)

    def ps(b, lo, hi, st=1, p=128):
        return ("PS%d" % b, lo, hi, st, p)

    def dd(i):
        return ("DB", 15 - i, 143 - i)

    PI, PG, PP = ("PCF", 0, 1), ("PCF", 1, 2), ("PCF", 2, 3)
    E16 = ("M16", 0, 16)
    IDN, BO = ("IDN", 0, 128), ("BO", 0, 128)

    dma("a", [(T.SIN[:, 0:16], T.bk[:, :]), (T.SIN[:, 16:48], T.qc[:, :]), (T.SIN[:, 48:80], T.qs[:, :])], ("SIN", 0, 80), [])
    dma("s", [(T.SIN[:, 80:83], T.ex[:, :]), (T.SIN[:, 83:89], T.zs[:, :])], ("SIN", 80, 89), [])
    cuts = [sum(CHUNKS[:c]) for c in range(len(CHUNKS) + 1)]
    for lo, hi in zip(cuts, cuts[1:]):
        dma("s", [(T.MT[:, lo:hi], T.mt[:, lo:hi])], ("MT", lo, hi), [])
    iota(("PCI", 2, 3), [[0, 1]], 0, 1)
    iota(("CLI", 0, 6), [[3, 3], [1, 2]], 1, 0)
    iota(("G16", 0, 128), [[16, 8], [0, 16]], 0, 0)
    iota(("C16", 0, 128), [[0, 8], [1, 16]], 0, 0)
    send(owner, ("LIN", 0, 89), ("SIN", 0, 89))
    iota(("PRI", 0, 128), [[0, 128]], 1, 0)
    pick(IDN, ("PRI", 0, 128), [[-1, 128]], Alu.is_equal, 1)
    iota(("J16", 0, 16), [[16, 16]], 0, 0)
    fill("ZE", 0, 4224)
    ms(("DB", 0, 144), 0.0)
    ms(("INC", 0, 1), 16.0 * U)
    ts(("PCI", 0, 1), ("PCI", 2, 3), 15, None, Alu.bitwise_and)
    ts(("PCI", 1, 2), ("PCI", 2, 3), 112, None, Alu.bitwise_and)
    cp(("PCF", 0, 3), ("PCI", 0, 3))
    cp(("CLU", 0, 6), ("CLI", 0, 6))
    lin(("XE", 0, 1), PI, 128.0, PG)
    for s, o in enumerate((2176.0, 2304.0, 2048.0)):
        lin(("OFF", 2 * s + 1, 2 * s + 2), ("XE", 0, 1), 1.0, o)
    cp(("OFF", 6, 7), PP)
    ts(BO, ("G16", 0, 128), PG, None, Alu.is_equal)
    ts(("M16", 0, 128), ("C16", 0, 128), PI, None, Alu.is_equal)
    fill("ZA", 0, 4352)
    cp(("DB", 15, 143, 16), ("BO", 0, 128, 16), "av")
    lin(("BON", 0, 128), BO, -1.0, 0.0)
    pick(("TRI", 0, 128), BO, [[1, 128]], Alu.is_gt, -1)
    fill1(("ZQ", 0, 1024), 0)
    fill1(("ZQ", 1024, 2048), 0)
    iota(("ZOI", 0, 8), [[128, 8]], 0, 1)
    cp(("ZOU", 0, 8), ("ZOI", 0, 8))
    fill("NAT", 0, 784, 256)
    iota(("NR", 0, 256), [[1, 256]], 0, 0)
    fill("GQ", 256, 272)
    fill("ZB", 0, 4096)
    fill("SA", 272, 288, -1)
    fill("TQ", 256, 272, -1)
    fill("TS", 256, 272, -1)
    fill("KS", 528, 1552, -1)
    fill("FIN", 528, 1552, -1)
    fill("WD", 0, 144)
    fill("FL", 48, 52)
    lin(("NN", 0, 16), ("J16", 0, 16), 1.0, PI)
    lin(("CB", 0, 16), ("NN", 0, 16), 1.0 / 512, 256.0)
    for t, top in ((0, 272.0), (1, 512.0)):
        lin(("SLN", 16 * t, 16 * t + 16), ("NN", 0, 16), -1.0, -top)
        lin(("SLU", 16 * t, 16 * t + 16), ("NN", 0, 16), U, top * U)
    lin(("TK", 0, 1), PI, 1.0 / 8192, 1000.0)
    lin(("EF", 0, 2), ("M16", 0, 2), -1.0, 1.0)
    lin(("TK2", 0, 1), PI, 1.0 / 8192, 0.0)
    lin(("TBC", 0, 16), E16, ("TK2", 0, 1), 0.0)
    lin(("KC", 0, 128), dd(0), ("TK", 0, 1), -1000.0)
    lin(("IM", 0, 128), IDN, ("EF", 0, 1), 0.0)
    lin(("KC", 128, 136), ("BO", 0, 128, 16), ("TK", 0, 1), -1000.0)

    for lo, hi in zip(PASS, PASS[1:]):
        lin(("NX", lo, hi), ("MT", lo, hi), 0.0625, -0.46875)
        ts(("MT", lo, hi), ("MT", lo, hi), 15, None, Alu.bitwise_and)

    cp(("LU", 0, 48), ("LIN", 0, 48), "va")
    cp(("WF", 0, 25), ("LIN", 64, 89), "va")
    ts(("KI", 0, 16), ("LIN", 48, 64), 6, None, Alu.arith_shift_right)
    cp(("KU", 0, 16), ("KI", 0, 16), "va")
    cp(("MSK", 0, 256), ind(E16, ("LU", 16, 32)), "av")
    cp(("MSK", 256, 512), ind(E16, ("LU", 32, 48)), "av")
    lin(("SP", 0, 16), ("WF", 0, 16), 0.125, 0.0)
    cp(("REC", 0, 16), ("WF", 3, 19), "gav")
    cp(("SA", 0, 16), ("WF", 6, 22), "gav")
    cp(("KS", 0, 16), ("WF", 9, 25), "gav")
    ZS = (("ZE", 2176, 4224), ("ZA", 2304, 4352), ("ZB", 2048, 4096))
    tt(("RL", 0, 96), ind(("WF", 16, 25), ("CLU", 0, 6)), ("M16", 0, 96), Alu.mult)
    acc(ps(2, 256, 352), [(BO, ("RL", 0, 96))])
    ts(("BL", 0, 96), ps(2, 256, 352), PI, None, Alu.is_equal)
    lin(("OFF", 0, 6, 2), ("WF", 16, 25, 3), 128.0, PP, "va")
    for s in range(3):
        cp(ind((ZS[s][0], 0, ZS[s][2]), ("OFF", 2 * s, 2 * s + 2)), ("BL", 32 * s, 32 * s + 32))
    cp(ind(("ZA", 2176, 2304), ("OFF", 6, 7)), ("BL", 48, 64))
    WNX, WOT = ("NX", 0, 4096), ("MT", 0, 4096)

    def step1(lst, k0, keep):
        cp(("G1U", k0, k0 + 256), ind(WNX, lst), "va")
        if keep is not None:
            lin(keep, ("G1U", k0, k0 + 256), 1.0, -2048.0)

    def queries(t):
        tt(("HM", 256 * t, 256 * t + 256), ind(("KG", 0, 256 * (t + 1)), ("KU", 16 * t, 16 * t + 16)), ("MSK", 256 * t, 256 * t + 256), Alu.mult)
        acc(ps(2, 0, 16), [(dd(i), ("HM", 256 * t + i, 256 * t + 256, 16)) for i in range(16)])
        lin(("QU", 16 * t, 16 * t + 16), ps(2, 0, 16), 1.0, 2048.0, "va")
        step1(("QU", 16 * t, 16 * t + 16), 256 * (t + 1), ("GQ", 0, 256) if t == 0 else None)

    def dest(s, k):
        if s == 0:
            return ("REC", 16 + k) if k < 512 else ("RQ1", k - 512)
        if s == 1:
            return ("SA", 16 + k if k < 256 else 32 + k)
        return (("KS", 16 + k), ("TS", k - 256), ("OWN", k - 512))[k // 256]

    def pick2(s, k0, w, b):
        x0 = (0, 768, 1280)[s] + k0
        for u in range(0, w, PW):
            v = min(u + PW, w)
            acc(ps(b, u, v), [((ZS[s][0], 128 * a, 128 * a + 128), ("G2", 16 * (k0 + u) + a, 16 * (k0 + v), 16)) for a in range(16)])
        lin(("X3", x0, x0 + w), ps(b, 0, w), 1.0, 2048.0, "va")

    def pick3(s, k0, subs, b):
        x0 = (0, 768, 1280)[s] + k0
        y0 = (k0 % 512, 512 + k0, 1024 + k0)[s]
        w = 0
        for sub in subs:
            cp(("G3", 16 * (y0 + w), 16 * (y0 + w + sub)), ind(WOT, ("X3", x0 + w, x0 + w + sub)), "av")
            w += sub
        z, o = ZS[s][:2]
        if b > 9:
            b -= 10
            t0 = 256 * (cnt["w"] % 2)
            cnt["w"] += 1
            for u in range(0, w, 128):
                for h in (0, 8):
                    mm([(ps(b, 256 + u + e, 384 + u, 16), ("G3", 16 * (y0 + u) + e, 16 * (y0 + u + 128), 16),
                         (z, o + 128 * e, o + 128 * e + 128, 16), True, True) for e in range(h, h + 8)])
            cp(("TB", t0, t0 + w), ps(b, 256, 256 + w), "av")
            mm([(ps(b, u, u + 128), ("TB", t0 + u, t0 + u + 128), IDN, True, True) for u in range(0, w, 128)])
        else:
            for u in range(0, w, PW):
                v = min(u + PW, w)
                acc(ps(b, u, v), [((z, o + 127 * e, o + 127 * e + 128), ("G3", 16 * (y0 + u) + e, 16 * (y0 + v), 16)) for e in range(16)])
        d, c0 = dest(s, k0)
        cp((d, c0, c0 + w), ps(b, 0, w), "av")

    def walks(plan):
        for s, k0, x, b in plan:
            if s < 0:
                lin(("G2", 16 * k0, 16 * (k0 + x)), ind(WNX, ("G1U", k0, k0 + x)), 1.0, -2048.0, "va")
            elif isinstance(x, int):
                pick2(s, k0, x, b)
            else:
                pick3(s, k0, x, b)

    def known_side(t, src, sq):
        n = 256 * (t + 1)
        square((sq, 15, 16 + n), (src, 15, 16 + n))
        acc(ps(7, 0, n), [(BO, (sq, 16, 16 + n)), (("BON", 0, 128), (sq, 15, 15 + n))])
        lin(("DBT", 512 * t, 512 * t + n), ps(7, 0, n), 1.0, U)
        if t == 0:
            pick(("DBT", 256, 512), ("DBT", 0, 256), [[1, 256]], Alu.is_gt, 0, -1.0e9)
        acc(ps(7, 0, 2), [(BO, (sq, 14 + n, 16 + n))])

    def match(t, rq, sq, known):
        n = 256 * (t + 1)
        c = (16 * t, 16 * t + 16)
        for lo in (0, 128):
            cp(ind(("ZQ", 8 * lo, 8 * lo + 1024), ("ZOU", 0, 8)), (rq[0], rq[1] + lo, rq[1] + lo + 128))
        square(sq, rq)
        acc(ps(2, 0, 16), [(dd(i), (sq[0], sq[1] + i, sq[2], 16)) for i in range(16)])
        ts(("UP",) + c, ps(2, 0, 16), ps(7, 1, 2), (n - 1) * U, Alu.add, Alu.add)
        m = 512 // n
        for j in range(0, 16, m):
            b = MB[j // m % len(MB)]
            mm([(ps(b, n * i, n * i + n), ("ZQ", 128 * (j + i), 128 * (j + i + 1)), (known, 16, 16 + n), True, True) for i in range(m)])
            scan(("SCN", n * j, n * j + 512), ("DBT", 512 * t, 512 * t + 512), ps(b, 0, 512), -1.0e9, Alu.add, Alu.max)
        tt(("TT",) + c, ("UP",) + c, ("SCN", n - 1, 16 * n, n), Alu.subtract)
        ts(("CMU",) + c, ("TT",) + c, 2048.0, float(n), Alu.mult, Alu.min)

    def places(t):
        c = (16 * t, 16 * t + 16)
        i0 = 18 * t
        ts(("NEW",) + c, ("TT",) + c, 0.4, U, Alu.is_ge, Alu.mult)
        scan(("INC", i0 + 1, i0 + 17), ("NEW",) + c, ("NEW",) + c, 16.0 * U if t == 0 else ("C1", 0, 1), Alu.add, Alu.max)
        tt(("NS",) + c, ("NEW",) + c, ("SLN",) + c, Alu.mult)
        p = ps(2, 0, 16)
        mm([(ps(2, 0, 17), BO, ("INC", i0, i0 + 17), True, False), (p, IDN, ("SLU",) + c, False, False),
            (p, ("TRI", 0, 128), ("NEW",) + c, False, False), (p, IDN, ("NS",) + c, False, True)])
        lin((("SCU", "RSU")[t], 0, 16), p, 2048.0, -256.0, "va")
        if t == 0:
            ts(("KI", 16, 32), ("SP", 0, 16), ps(2, 16, 17), -0.499969482421875, Alu.mult, Alu.add)
            cp(("KU", 16, 32), ("KI", 16, 32), "va")
            lin(("C1", 0, 1), ps(2, 16, 17), 1.0 / 16, 0.0)
            cp(("INC", 18, 19), ("C1", 0, 1), "av")
        else:
            cp(("MSG", 32, 48), p, "va")
        tt(("MSG",) + c, ("TT",) + c, p, Alu.min)

    def winner(t, src, own):
        n = 256 * (t + 1)
        ne = ("NE", 256 * t, 256 * t + 256)
        tt(ne, ind((src, 16, 32 + n), ("CMU", 16 * t, 16 * t + 16)), own, Alu.not_equal)
        count(("NC", t, t + 1), ne)
        lin(("RH", 16 * t, 16 * t + 16), E16, ("NC", t, t + 1), 0.0, "va")
        acc(ps(7, 0, 16), [(BO, ("RH", 16 * t, 16 * t + 16)), (BO, ("TBC", 0, 16))])
        red(("MN", t, t + 1), ps(7, 0, 16), Alu.min)
        ts((("WS", 0, 128), ("WD", 15, 143, 16))[t], ("KC", 128 * t, (128, 136)[t]), ("NC", t, t + 1), ("MN", t, t + 1), Alu.add, Alu.is_equal)

    step1(("LU", 0, 16), 0, ("KG", 0, 256))
    queries(0)
    walks(PA)
    known_side(0, "REC", "SQ0")
    walks(PA2)
    match(0, ("REC", 272, 528), ("SQ0", 272, 528), "REC")
    places(0)
    send(client, ("RMS", 0, 16), ("MSG", 0, 16))
    cp(ind(("NAT", 0, 784), ("SCU", 0, 16)), ("NR", 0, 256))
    acc(ps(2, 0, 16), [(dd(i), ("NAT", i, 256, 16)) for i in range(16)])
    lin(("NL", 0, 16), ps(2, 0, 16), 1.0 / 16, 0.0, "va")
    cp(("KG", 256, 512), ind(("GQ", 0, 272), ("NL", 0, 16)), "av")
    walks(PB)
    queries(1)
    winner(0, "SA", ("SA", 288, 544))
    ts(("PJ", 0, 9), ("CB", 0, 9), ("MN", 0, 1), 8192.0, Alu.add, Alu.mult)
    ts(("PJ", 10, 19), ("PJ", 0, 9), 8191, None, Alu.bitwise_and)
    cp(("PU", 0, 9), ("PJ", 10, 19), "va")
    cp(("ZE", 0, 2304, 16), ind(("ZA", 0, 2304), ("PU", 0, 9)), "va")
    acc(ps(7, 0, 256), [(("IM", 0, 128), ("REC", 272, 528)), (("WS", 0, 128), ("SA", 288, 544))])
    cp(("TQ", 0, 256), ps(7, 0, 256), "av")
    acc(ps(7, 0, 272), [(("IM", 0, 128), ("REC", 0, 272)), (("WS", 0, 128), ("SA", 0, 272))])
    cp(("KR", 0, 272), ps(7, 0, 272), "av")
    cp(("KR", 272, 528), ind(("TQ", 0, 272), ("NL", 0, 16)), "av")
    known_side(1, "KR", "SQ1")
    send(client, ("RKR", 0, 528), ("KR", 0, 528))
    walks(PC)
    cp(("KS", 272, 528), ind(("TS", 0, 272), ("NL", 0, 16)), "av")
    walks(PD)
    send(client, ("RQ", 0, 256), ("RQ1", 0, 256))
    walks(PE)
    match(1, ("RQ1", 0, 256), ("SQQ", 0, 256), "KR")
    places(1)
    send(client, ("RMS", 16, 48), ("MSG", 16, 48))
    winner(1, "KS", ("OWN", 0, 256))
    cp(ind(("KS", 272, 1552), ("RSU", 0, 16)), ("OWN", 0, 256))
    acc(ps(3, 0, 48), [(("WD", 15 - i, 143 - i), ("KS", 16 + 48 * i, 64 + 48 * i)) for i in range(16)])
    cp(("FL", 0, 48), ps(3, 0, 48), "av")
    acc(ps(4, 0, 4, 1, 8), [(("WD", 15, 143, 16), ("KS", 12, 16))])
    cp(("FL", 48, 52, 1, 8), ps(4, 0, 4, 1, 8), "va")
    send(client, ("RFL", 0, 52), ("FL", 0, 52))
    cp(("FIN", 12, 272), ("RKR", 12, 272), "gav")
    cp(("FIN", 272, 528), ("RKR", 272, 528), "gav")
    lin(("RSU", 16, 32), ("RMS", 32, 48), 2048.0, -256.0, "va")
    cp(ind(("FIN", 272, 1552), ("RSU", 16, 32)), ("RQ", 0, 256))
    mm([(ps(7, i, 512, 16, 8), ("IDN", i, 128, 16), ("RMS", 0, 32), True, True) for i in range(16)])
    lin(("YM", 0, 512, 1, 8), ps(7, 0, 512, 1, 8), 2048.0, 0.0)
    dma("s", [(T.ym[:, :], T.YM[0:8, :])], ("ym", 0, 512), [("YM", 0, 512)])
    rows = [(0, 1)] + [(16 * k + 2, min(16 * k + 17, 128)) for k in range(8)]
    dma("s", [(T.yr[a:b, 0:256], T.FIN[a:b, 16:272]) for a, b in rows], ("yr0", 0, 1), [("FIN", 16, 272)])
    for q, part in (("s", rows[:5]), ("a", rows[5:])):
        dma(q, [(T.yr[a:b, 256:768], T.FIN[a:b, 272:784]) for a, b in part], ("yr" + q, 0, 1), [("FIN", 272, 784)])
    dma("s", [(T.ye[a:b, :], T.FIN[a:b, 13:16]) for a, b in rows], ("ye0", 0, 1), [("FIN", 12, 16)])
    dma("s", [(T.yr[1:128:16, :], T.RFL[:, 0:48]), (T.ye[1:128:16, :], T.RFL[0:8, 49:52])], ("yr1", 0, 1), [("RFL", 0, 52)])
    return ops


def deps(ops):
    pred = [dict() for _ in ops]
    seen = {}
    for i, o in enumerate(ops):
        use = [(r, True) for r in o["w"]] + [(r, False) for r in o["r"]]
        for r, wr in use:
            lst = seen.get(r[0], [])
            if r[0].startswith("PS"):
                if lst and lst[-1][0] != i:
                    pred[i].setdefault(lst[-1][0], False)
            else:
                for j, lo, hi, w2 in lst:
                    if j != i and lo < r[2] and r[1] < hi and (wr or w2):
                        pred[i][j] = True
        for r, wr in use:
            seen.setdefault(r[0], []).append((i, r[1], r[2], wr))
    return pred


def rank_program(g, core, T, topo):
    if T.rank_of(core) is None:
        return
    ops = build(T, topo, core)
    pred = deps(ops)
    seq = []
    for x in ORDER.split():
        i = int(x.rstrip("vag"))
        ops[i]["on"] = x[-1] if x[-1] in "vag" else ops[i]["eng"][0]
        seq.append(i)
    pos = {i: k for k, i in enumerate(seq)}
    assert sorted(seq) == list(range(len(ops)))
    known = {e: {} for e in "vapgs"}
    clock, waits, wanted = {}, {}, set()
    for i in seq:
        e = ops[i]["on"]
        kn = known[e]
        waits[i] = []
        for j in sorted(pred[i], key=lambda j: -pos[j]):
            assert pos[j] < pos[i]
            w = pred[i][j]
            pj = ops[j]
            if pj["on"] == e and pj["kind"] == "c" and (not w or e == "p"):
                continue
            key = pj["on"] if pj["kind"] == "c" else pj["sem"]
            if kn.get(key, -1) >= pos[j]:
                continue
            waits[i].append(j)
            wanted.add(j)
            kn[key] = pos[j]
            if pj["kind"] != "r":
                for k2, v2 in clock[j].items():
                    if kn.get(k2, -1) < v2:
                        kn[k2] = v2
        clock[i] = dict(kn)
    count, total = {}, {e: 0 for e in "vapgs"}
    for i in seq:
        if ops[i]["kind"] == "c" and i in wanted:
            total[ops[i]["on"]] += 1
            count[i] = total[ops[i]["on"]]
    queue = {"v": g.vector, "a": g.scalar, "p": g.tensor, "g": g, "s": g.sync}
    sent = 0
    for i in seq:
        o = ops[i]
        q = queue[o["on"]]
        for j in waits[i]:
            pj = ops[j]
            if pj["kind"] == "c":
                q.wait_ge(T.sem["c" + pj["on"]], count[j])
            else:
                q.wait_ge(T.sem[pj["sem"]], pj["n"])
        x = o["fn"](q, o["on"])
        if i in count:
            x.then_inc(T.sem["c" + o["on"]], 1)
        if o["kind"] == "r":
            sent += o["n"]
    g.wait_ge(T.sem.lsem, sent)
    for i in seq:
        if ops[i]["kind"] == "d" and i not in wanted:
            g.sync.wait_ge(T.sem[ops[i]["sem"]], ops[i]["n"])
